import numpy as np
import ml_dtypes


def mxq(x, axis, fmt="e4m3"):
    dtype, down = {"e4m3": (ml_dtypes.float8_e4m3fn, 7), "e5m2": (ml_dtypes.float8_e5m2, 14)}[fmt]
    v = np.moveaxis(np.asarray(x, np.float32).astype(ml_dtypes.bfloat16).astype(np.float64), axis, -1)
    blocks = v.reshape(v.shape[:-1] + (-1, 32))
    amax = np.abs(blocks).max(-1, keepdims=True)
    byte = np.maximum(np.where(amax > 0, np.frexp(amax)[1] - 1 + 127, 0) - down, 1)
    scale = np.exp2(byte - 127.0)
    codes = (blocks / scale).astype(np.float32).astype(dtype).astype(np.float64)
    return np.moveaxis((codes * scale).reshape(v.shape), -1, axis)


WIDE = False


def mx_kscale(k):
    if not WIDE:
        return np.ones(k)
    levels = np.array([10, -10, 5, -5, 0])
    if k % 512:
        return np.exp2(np.random.permutation(np.resize(levels, k // 32))).repeat(32)
    a = np.empty((k // 512, 16))
    for p in range(k // 512):
        a[p, :8] = np.random.permutation(np.resize(levels, 8))
        for g in range(8):
            far = levels[np.abs(levels - a[p, g]) >= 10]
            a[p, g + 8] = far[np.random.randint(len(far))]
    return np.exp2(a.ravel()).repeat(32)


def f64(x):
    return np.asarray(x).astype(np.float64)


def striped(idx):
    return np.tile(idx.reshape(-1, 16).T, (8, 1)).astype(np.uint16)


def unstriped(offs):
    return offs[:16].T.reshape(-1).astype(np.int64)


E2M1 = np.array([0.0, 0.5, 1.0, 1.5, 2.0, 3.0, 4.0, 6.0, -0.0, -0.5, -1.0, -1.5, -2.0, -3.0, -4.0, -6.0])


def pack_fp4(w):
    k, n = w.shape
    w = f64(np.asarray(w, np.float32).astype(ml_dtypes.bfloat16)).reshape(k // 32, 32, n)
    amax = np.abs(w).max(1)
    mant, ex = np.frexp(amax / 6.0)
    byte = np.clip(np.where(amax > 0, np.where(mant > 0.5, ex, ex - 1) + 127, 1), 1, 254)
    scaled = (w * np.exp2(127.0 - byte)[:, None, :]).reshape(k, n).astype(np.float32)
    c = np.ascontiguousarray(scaled.reshape(k // 512, 128, 4, n).transpose(0, 1, 3, 2)).astype(ml_dtypes.float4_e2m1fn).view(np.uint8) & 0xF
    words = (c[..., 0::2] | (c[..., 1::2] << 4)).reshape(k // 512, 128, 2 * n)
    return np.ascontiguousarray(words), np.ascontiguousarray(byte.astype(np.uint8).reshape(k // 512, 16, n))


def unpack_fp4(words, scales):
    g, _, n = scales.shape
    words = np.ascontiguousarray(words).reshape(g, 128, n, 2)
    nib = np.empty((g, 128, n, 4), np.uint8)
    nib[..., 0::2] = words & 0xF
    nib[..., 1::2] = words >> 4
    vals = E2M1[nib] * np.repeat(np.exp2(scales.astype(np.float64) - 127.0), 8, axis=1)[..., None]
    return vals.transpose(0, 1, 3, 2).reshape(g * 512, n)


def relu(v):
    return np.maximum(v, 0.0)


def gelu(v):
    return 0.5 * v * (1.0 + np.tanh(np.sqrt(2.0 / np.pi) * (v + 0.044715 * v**3)))


K, T, S, D, V, H, N, U = 512, 4096, 1024, 2, 512, 512, 256, 256
P = 2 ** 7


def setup_inputs():
    n = np.random.standard_normal
    s = mx_kscale(K)[:, None]
    u = mx_kscale(H)
    packed_xT = pack_fp4(n((K, T)) * s)
    return {
        "x_words": packed_xT[0],
        "x_scales": packed_xT[1],
        "w1": (n((K, H)) / np.sqrt(K) / s * u).astype(np.float32),
        "w2": (n((H, N)) / np.sqrt(H) / u[:, None]).astype(np.float32),
        "gate": (np.tile(np.random.uniform(0.2, 1.0, (D, 1, V)) / np.sqrt(D), (1, P, 1))).astype(np.float32),
        "gate2": (np.tile(np.random.uniform(0.2, 1.0, (D, 1, U)) / np.sqrt(D), (1, P, 1))).astype(np.float32),
        "offs": striped(np.random.permutation(T)[:S]),
        "pos1": striped(np.random.permutation(S)[:V]),
        "pos2": striped(np.random.permutation(S)[:V]),
        "nxt1": striped(np.random.permutation(V)[:U]),
        "nxt2": striped(np.random.permutation(V)[:U]),
    }


def reference(x_words, x_scales, w1, w2, gate, gate2, offs, pos1, pos2, nxt1, nxt2):
    xq = unpack_fp4(x_words, x_scales)[:, unstriped(offs)]
    h = gelu(mxq(f64(w1), 0, "e4m3").T @ xq)
    z = h[:, unstriped(pos1)] * f64(gate)[0, :1] + h[:, unstriped(pos2)] * f64(gate)[1, :1]
    g = relu(mxq(f64(w2), 0, "e4m3").T @ mxq(z, 0, "e4m3"))
    return g[:, unstriped(nxt1)] * f64(gate2)[0, :1] + g[:, unstriped(nxt2)] * f64(gate2)[1, :1]

@@ -1,0 +1,227 @@
+from contextlib import ExitStack
+
+import concourse.mybir as mybir
+from concourse.masks import make_identity
+
+K, T, S, V, H, N, U = 512, 4096, 1024, 512, 512, 256, 256
+FLOPS = 2 * K * H * S + 2 * H * N * V
+
+F32 = mybir.dt.float32
+BF16 = mybir.dt.bfloat16
+I32 = mybir.dt.int32
+U32 = mybir.dt.uint32
+U16 = mybir.dt.uint16
+U8 = mybir.dt.uint8
+FP8X4 = mybir.dt.float8_e4m3fn_x4
+FP4X4 = mybir.dt.float4_e2m1fn_x4
+ACT = mybir.ActivationFunctionType
+MULT = mybir.AluOpType.mult
+ADD = mybir.AluOpType.add
+
+P = 128
+HALF = 512
+
+
+def tile_picked_hop2_gelu_p_kernel(
+    tc, x_words, x_scales, w1, w2, gate, gate2, offs, pos1, pos2, nxt1, nxt2, out
+):
+    nc = tc.nc
+    with ExitStack() as ctx:
+        keep = ctx.enter_context(tc.tile_pool(name="keep", bufs=1))
+        ring = ctx.enter_context(tc.tile_pool(name="ring", bufs=1))
+        psum = ctx.enter_context(tc.psum_pool(name="psum", bufs=1))
+
+        def held(shape, dtype, name):
+            return keep.tile(shape, dtype, name=name, align_bytes=64)
+
+        offs_sb = held([P, S // 16], U16, "offs_sb")
+        pos_sb = [held([P, V // 16], U16, "pos%d" % d) for d in range(2)]
+        nxt_sb = [held([P, U // 16], U16, "nxt%d" % d) for d in range(2)]
+        words_all = held([P, T], U16, "words_all")
+        scales_all = ring.tile([P, T], U8, name="scales_all", tag="table", bufs=1, align_bytes=64)
+        w1_raw = [held([P, 4, H // 2], F32, "w1_raw%d" % i) for i in range(2)]
+        w2_raw = held([P, 4, N], F32, "w2_raw")
+        gate_main = ring.tile([P, 2, 3 * P], F32, name="gate_main", tag="last", bufs=1, align_bytes=64)
+        gate_last = held([P, 2, P], F32, "gate_last")
+        gate2_sb = held([P, 2, U], F32, "gate2_sb")
+        ident = held([P, P], F32, "ident")
+
+        nc.vector.memset(scales_all[:].bitcast(I32), 0)
+        w1_rows = w1.rearrange("(p j) n -> p j n", j=4)
+        nc.sync.dma_start(offs_sb[:], offs)
+        nc.sync.dma_start(words_all[:].bitcast(I32), x_words[0].bitcast(I32))
+        scale_words = x_scales[0].bitcast(I32)
+        for q in range(4):
+            nc.sync.dma_start(scales_all[32 * q : 32 * q + 4, :].bitcast(I32), scale_words[4 * q : 4 * q + 4, :])
+        for i in range(2):
+            nc.sync.dma_start(w1_raw[i][:], w1_rows[:, :, 256 * i : 256 * (i + 1)])
+        nc.sync.dma_start(pos_sb[0][:], pos1)
+        nc.sync.dma_start(pos_sb[1][:], pos2)
+        nc.sync.dma_start(nxt_sb[0][:], nxt1)
+        nc.sync.dma_start(nxt_sb[1][:], nxt2)
+        gate_rows = gate.rearrange("d p v -> p d v")
+        nc.sync.dma_start(gate_main[:], gate_rows[:, :, : 3 * P])
+        nc.sync.dma_start(w2_raw[:], w2.rearrange("(p j) n -> p j n", j=4))
+        nc.sync.dma_start(gate_last[:], gate_rows[:, :, 3 * P :])
+        nc.sync.dma_start(gate2_sb[:], gate2.rearrange("d p r -> p d r"))
+        make_identity(nc, ident[:])
+        warm = held([P, 8], F32, "warm")
+        nc.gpsimd.memset(warm[:, :1], 0.0)
+        nc.scalar.activation(warm[:, 4:5], warm[:, :1], ACT.Gelu_apprx_tanh)
+
+        def quantise(grouped, width, name):
+            codes = held([P, width], U32, name + "_codes")
+            scales = held([P, width], U8, name + "_scales")
+            nc.vector.quantize_mx(out=codes[:].bitcast(FP8X4), scales=scales[:], in_=grouped)
+            return codes, scales
+
+        w1_first = ring.tile([P, 4 * P], BF16, name="w1_first", tag="first", bufs=1, align_bytes=64)
+        w1_rest = held([P, 3 * 4 * P], BF16, "w1_rest")
+        for i in range(2):
+            raw = w1_raw[i][:].rearrange("p j (m t) -> p m j t", t=4)
+            nc.scalar.copy(w1_first[:].rearrange("p (m j) -> p m j", j=4)[:, 64 * i : 64 * (i + 1), :], raw[:, :, :, 0])
+            nc.scalar.copy(
+                w1_rest[:].rearrange("p (t m j) -> p m j t", t=3, j=4)[:, 64 * i : 64 * (i + 1), :, :], raw[:, :, :, 1:]
+            )
+
+        x_codes, x_exps = [], []
+        for half in range(2):
+            codes = held([P, HALF], U16, "x_codes%d" % half)
+            nc.vector.tensor_copy(codes[:], words_all[:].indirect(offs_sb[:, 32 * half : 32 * half + 32]))
+            x_codes.append(codes)
+        exps = held([P, HALF], U8, "x_exps0")
+        nc.vector.tensor_copy(exps[:], scales_all[:].indirect(offs_sb[:, :32]))
+        x_exps.append(exps)
+        w1_q = [quantise(w1_first[:], P, "w1_0")]
+        exps = ring.tile([P, HALF], U8, name="x_exps1", tag="first", bufs=1, align_bytes=64)
+        nc.vector.tensor_copy(exps[:], scales_all[:].indirect(offs_sb[:, 32:]))
+        x_exps.append(exps)
+        rest_codes = ring.tile([P, 3 * P], U32, name="rest_codes", tag="table", bufs=1, align_bytes=64)
+        rest_scales = held([P, 3 * P], U8, "rest_scales")
+        for t in range(3):
+            cols = slice(P * t, P * (t + 1))
+            nc.vector.quantize_mx(
+                out=rest_codes[:, cols].bitcast(FP8X4), scales=rest_scales[:, cols], in_=w1_rest[:, 4 * P * t : 4 * P * (t + 1)]
+            )
+            w1_q.append((rest_codes[:, cols], rest_scales[:, cols]))
+
+        def bank(shape):
+            return psum.tile(shape, F32, name="bank", tag="bank", bufs=5)
+
+        h = []
+        for t in range(4):
+            h_t = held([P, S], F32, "h%d" % t)
+            codes, scales = w1_q[t]
+            pieces = [(0, 512), (512, 256), (768, 256)] if t == 0 else [(0, 512), (512, 512)]
+            for c0, width in pieces:
+                acc = bank([P, width])
+                cols = slice(c0 % HALF, c0 % HALF + width)
+                nc.tensor.matmul_mx(
+                    out=acc[:],
+                    lhsT=codes[:].bitcast(FP8X4),
+                    lhsT_scale=scales[:],
+                    rhs=x_codes[c0 // HALF][:, cols].bitcast(FP4X4),
+                    rhs_scale=x_exps[c0 // HALF][:, cols],
+                    start=True,
+                    stop=True,
+                )
+                nc.scalar.activation(h_t[:, c0 : c0 + width], acc[:], ACT.Gelu_apprx_tanh)
+            h.append(h_t)
+
+        w2_grouped = held([P, N, 4], BF16, "w2_grouped")
+        nc.vector.tensor_copy(
+            w2_grouped[:].rearrange("p (c i) j -> p c j i", i=4), w2_raw[:].rearrange("p j (c i) -> p c j i", i=4)
+        )
+        w2_codes, w2_scales = quantise(w2_grouped[:].rearrange("p n j -> p (n j)"), N, "w2")
+
+        z_sum = [psum.tile([P, H], F32, name="z_sum%d" % b) for b in range(3)]
+        z_rows = [held([P, 2, P, 2], BF16, "z_rows%d" % b) for b in range(3)]
+
+        def gather(dst, t, d, v0, width, weights):
+            nc.vector.tensor_tensor(dst, h[t][:].indirect(pos_sb[d][:, v0 // 16 : (v0 + width) // 16]), weights, MULT)
+
+        def gather_and_turn(t, v0, width):
+            parts = []
+            for d in range(2):
+                part = held([P, width], F32, "part%d_%d_%d" % (t, v0, d))
+                gather(part[:], t, d, v0, width, gate_main[:, d, v0 : v0 + width])
+                parts.append(part)
+            for b in range(v0 // P, (v0 + width) // P):
+                for d in range(2):
+                    nc.tensor.matmul(
+                        z_sum[b][:, P * t : P * (t + 1)],
+                        parts[d][:, P * b - v0 : P * (b + 1) - v0],
+                        ident[:],
+                        start=(d == 0),
+                        stop=(d == 1),
+                        is_transpose=True,
+                    )
+
+        def round_rows(b, u):
+            nc.scalar.copy(
+                z_rows[b][:, u, :, :], z_sum[b][:, 2 * P * u : 2 * P * (u + 1)].rearrange("v (e p) -> v p e", e=2)
+            )
+
+        def turn_back(blocks, grouped):
+            turned = bank([P, len(blocks), 2, P])
+            for i, b in enumerate(blocks):
+                pairs = z_rows[b][:].rearrange("v u p e -> v (u p e)").bitcast(F32)
+                for u in range(2):
+                    nc.tensor.transpose(turned[:, i, u, :], pairs[:, P * u : P * (u + 1)], ident[:])
+            nc.scalar.copy(
+                grouped.bitcast(F32).rearrange("p (b v u) -> p b v u", v=P, u=2),
+                turned[:].rearrange("p b u v -> p b v u"),
+            )
+
+        g = [held([P, V], F32, "g%d" % m) for m in range(2)]
+
+        def second_layer(grouped, v0, width):
+            codes, scales = quantise(grouped, width, "z%d" % v0)
+            for m in range(2):
+                acc = bank([P, width])
+                nc.tensor.matmul_mx(
+                    out=acc[:],
+                    lhsT=w2_codes[:, P * m : P * (m + 1)].bitcast(FP8X4),
+                    lhsT_scale=w2_scales[:, P * m : P * (m + 1)],
+                    rhs=codes[:].bitcast(FP8X4),
+                    rhs_scale=scales[:],
+                    start=True,
+                    stop=True,
+                )
+                nc.scalar.activation(g[m][:, v0 : v0 + width], acc[:], ACT.Relu)
+
+        for t in range(2):
+            gather_and_turn(t, 0, 3 * P)
+        for b in range(3):
+            round_rows(b, 0)
+        gather_and_turn(2, 0, 3 * P)
+        gather_and_turn(3, 0, 2 * P)
+        gather_and_turn(3, 2 * P, P)
+        last = ring.tile([P, 10 * P], F32, name="last", tag="last", bufs=1, align_bytes=64)
+        for b in range(3):
+            round_rows(b, 1)
+        grouped = last[:, 6 * P :].bitcast(BF16)
+        turn_back([0, 1], grouped)
+        second_layer(grouped, 0, 2 * P)
+        for t in range(4):
+            for d in range(2):
+                c0 = (2 * t + d) * P
+                gather(last[:, c0 : c0 + P], t, d, 3 * P, P, gate_last[:, d, :])
+        grouped = ring.tile([P, 4 * P], BF16, name="grouped", tag="grouped", bufs=1, align_bytes=64)
+        turn_back([2], grouped[:])
+        second_layer(grouped[:], 2 * P, P)
+        grouped = ring.tile([P, 4 * P], BF16, name="grouped", tag="grouped", bufs=1, align_bytes=64)
+        terms = last[:, : 8 * P].rearrange("p (t d c i) -> p d c t i", t=4, d=2, i=4)
+        nc.vector.tensor_tensor(grouped[:].rearrange("p (c i t) -> p c t i", i=4, t=4), terms[:, 0], terms[:, 1], ADD)
+        second_layer(grouped[:], 3 * P, P)
+
+        terms = []
+        for m in range(2):
+            for d in range(2):
+                term = held([P, U], F32, "term%d%d" % (m, d))
+                nc.vector.tensor_tensor(term[:], g[m][:].indirect(nxt_sb[d][:]), gate2_sb[:, d, :], MULT)
+                terms.append(term)
+        for m in range(2):
+            result = held([P, U], F32, "result%d" % m)
+            nc.vector.tensor_tensor(result[:], terms[2 * m][:], terms[2 * m + 1][:], ADD)
+            nc.sync.dma_start(out[P * m : P * (m + 1), :], result[:])

@@ -38,35 +38,35 @@ def tile_picked_hop2_gelu_p_kernel(
         pos_sb = [held([P, V // 16], U16, "pos%d" % d) for d in range(2)]
         nxt_sb = [held([P, U // 16], U16, "nxt%d" % d) for d in range(2)]
         words_all = held([P, T], U16, "words_all")
-        scales_all = ring.tile([P, T], U8, name="scales_all", tag="table", bufs=1, align_bytes=64)
-        w1_raw = [held([P, 4, H // 2], F32, "w1_raw%d" % i) for i in range(2)]
+        scales_all = held([P, T], U8, "scales_all")
+        w1_raw = [held([P, 2, H], F32, "w1_raw%d" % i) for i in range(2)]
         w2_raw = held([P, 4, N], F32, "w2_raw")
         gate_main = ring.tile([P, 2, 3 * P], F32, name="gate_main", tag="last", bufs=1, align_bytes=64)
         gate_last = held([P, 2, P], F32, "gate_last")
         gate2_sb = held([P, 2, U], F32, "gate2_sb")
         ident = held([P, P], F32, "ident")
 
-        nc.vector.memset(scales_all[:].bitcast(I32), 0)
-        w1_rows = w1.rearrange("(p j) n -> p j n", j=4)
-        nc.sync.dma_start(offs_sb[:], offs)
-        nc.sync.dma_start(words_all[:].bitcast(I32), x_words[0].bitcast(I32))
+        nc.gpsimd.memset(scales_all[:].bitcast(I32), 0)
         scale_words = x_scales[0].bitcast(I32)
         for q in range(4):
-            nc.sync.dma_start(scales_all[32 * q : 32 * q + 4, :].bitcast(I32), scale_words[4 * q : 4 * q + 4, :])
-        for i in range(2):
-            nc.sync.dma_start(w1_raw[i][:], w1_rows[:, :, 256 * i : 256 * (i + 1)])
+            nc.gpsimd.dma_start(scales_all[32 * q : 32 * q + 4, :].bitcast(I32), scale_words[4 * q : 4 * q + 4, :])
+        w1_rows = w1.rearrange("(p j) n -> p j n", j=4)
+        nc.sync.dma_start(words_all[:].bitcast(I32), x_words[0].bitcast(I32))
+        nc.sync.dma_start(offs_sb[:], offs)
+        nc.sync.dma_start(w1_raw[0][:], w1_rows[:, :2, :])
+        nc.sync.dma_start(w1_raw[1][:], w1_rows[:, 2:, :])
         nc.sync.dma_start(pos_sb[0][:], pos1)
         nc.sync.dma_start(pos_sb[1][:], pos2)
-        nc.sync.dma_start(nxt_sb[0][:], nxt1)
-        nc.sync.dma_start(nxt_sb[1][:], nxt2)
         gate_rows = gate.rearrange("d p v -> p d v")
         nc.sync.dma_start(gate_main[:], gate_rows[:, :, : 3 * P])
         nc.sync.dma_start(w2_raw[:], w2.rearrange("(p j) n -> p j n", j=4))
         nc.sync.dma_start(gate_last[:], gate_rows[:, :, 3 * P :])
         nc.sync.dma_start(gate2_sb[:], gate2.rearrange("d p r -> p d r"))
+        nc.sync.dma_start(nxt_sb[1][:], nxt2)
+        nc.sync.dma_start(nxt_sb[0][:], nxt1)
         make_identity(nc, ident[:])
         warm = held([P, 8], F32, "warm")
-        nc.gpsimd.memset(warm[:, :1], 0.0)
+        nc.vector.memset(warm[:, :1], 0.0)
         nc.scalar.activation(warm[:, 4:5], warm[:, :1], ACT.Gelu_apprx_tanh)
 
         def quantise(grouped, width, name):
@@ -79,9 +79,9 @@ def tile_picked_hop2_gelu_p_kernel(
         w1_rest = held([P, 3 * 4 * P], BF16, "w1_rest")
         for i in range(2):
             raw = w1_raw[i][:].rearrange("p j (m t) -> p m j t", t=4)
-            nc.scalar.copy(w1_first[:].rearrange("p (m j) -> p m j", j=4)[:, 64 * i : 64 * (i + 1), :], raw[:, :, :, 0])
+            nc.scalar.copy(w1_first[:].rearrange("p (m j) -> p m j", j=4)[:, :, 2 * i : 2 * i + 2], raw[:, :, :, 0])
             nc.scalar.copy(
-                w1_rest[:].rearrange("p (t m j) -> p m j t", t=3, j=4)[:, 64 * i : 64 * (i + 1), :, :], raw[:, :, :, 1:]
+                w1_rest[:].rearrange("p (t m j) -> p m j t", t=3, j=4)[:, :, 2 * i : 2 * i + 2, :], raw[:, :, :, 1:]
             )
 
         x_codes, x_exps = [], []
@@ -96,14 +96,8 @@ def tile_picked_hop2_gelu_p_kernel(
         exps = ring.tile([P, HALF], U8, name="x_exps1", tag="first", bufs=1, align_bytes=64)
         nc.vector.tensor_copy(exps[:], scales_all[:].indirect(offs_sb[:, 32:]))
         x_exps.append(exps)
-        rest_codes = ring.tile([P, 3 * P], U32, name="rest_codes", tag="table", bufs=1, align_bytes=64)
-        rest_scales = held([P, 3 * P], U8, "rest_scales")
-        for t in range(3):
-            cols = slice(P * t, P * (t + 1))
-            nc.vector.quantize_mx(
-                out=rest_codes[:, cols].bitcast(FP8X4), scales=rest_scales[:, cols], in_=w1_rest[:, 4 * P * t : 4 * P * (t + 1)]
-            )
-            w1_q.append((rest_codes[:, cols], rest_scales[:, cols]))
+        for t in range(1, 4):
+            w1_q.append(quantise(w1_rest[:, 4 * P * (t - 1) : 4 * P * t], P, "w1_%d" % t))
 
         def bank(shape):
             return psum.tile(shape, F32, name="bank", tag="bank", bufs=5)

@@ -39,35 +39,34 @@ def tile_picked_hop2_gelu_p_kernel(
         nxt_sb = [held([P, U // 16], U16, "nxt%d" % d) for d in range(2)]
         words_all = held([P, T], U16, "words_all")
         scales_all = held([P, T], U8, "scales_all")
-        w1_raw = [held([P, 2, H], F32, "w1_raw%d" % i) for i in range(2)]
+        w1_raw = [held([P, 4, H // 2], F32, "w1_raw%d" % i) for i in range(2)]
         w2_raw = held([P, 4, N], F32, "w2_raw")
-        gate_main = ring.tile([P, 2, 3 * P], F32, name="gate_main", tag="last", bufs=1, align_bytes=64)
-        gate_last = held([P, 2, P], F32, "gate_last")
+        gate_main = ring.tile([P, 2, 2 * P], F32, name="gate_main", tag="last", bufs=1, align_bytes=64)
+        gate_last = held([P, 2, 2 * P], F32, "gate_last")
         gate2_sb = held([P, 2, U], F32, "gate2_sb")
         ident = held([P, P], F32, "ident")
 
-        nc.gpsimd.memset(scales_all[:].bitcast(I32), 0)
-        scale_words = x_scales[0].bitcast(I32)
-        for q in range(4):
-            nc.gpsimd.dma_start(scales_all[32 * q : 32 * q + 4, :].bitcast(I32), scale_words[4 * q : 4 * q + 4, :])
+        nc.vector.memset(scales_all[:].bitcast(I32), 0)
         w1_rows = w1.rearrange("(p j) n -> p j n", j=4)
-        nc.sync.dma_start(words_all[:].bitcast(I32), x_words[0].bitcast(I32))
         nc.sync.dma_start(offs_sb[:], offs)
-        nc.sync.dma_start(w1_raw[0][:], w1_rows[:, :2, :])
-        nc.sync.dma_start(w1_raw[1][:], w1_rows[:, 2:, :])
+        nc.sync.dma_start(words_all[:].bitcast(I32), x_words[0].bitcast(I32))
         nc.sync.dma_start(pos_sb[0][:], pos1)
         nc.sync.dma_start(pos_sb[1][:], pos2)
+        nc.sync.dma_start(w1_raw[0][:], w1_rows[:, :, :256])
+        scale_words = x_scales[0].bitcast(I32)
+        for q in range(4):
+            nc.sync.dma_start(scales_all[32 * q : 32 * q + 4, :].bitcast(I32), scale_words[4 * q : 4 * q + 4, :])
+        nc.sync.dma_start(nxt_sb[0][:], nxt1)
+        nc.sync.dma_start(w1_raw[1][:], w1_rows[:, :, 256:])
         gate_rows = gate.rearrange("d p v -> p d v")
-        nc.sync.dma_start(gate_main[:], gate_rows[:, :, : 3 * P])
-        nc.sync.dma_start(w2_raw[:], w2.rearrange("(p j) n -> p j n", j=4))
-        nc.sync.dma_start(gate_last[:], gate_rows[:, :, 3 * P :])
+        nc.sync.dma_start(gate_main[:], gate_rows[:, :, : 2 * P])
+        w2_rows = w2.rearrange("(b t r) n -> t b r n", t=4, r=8)
+        for t in range(4):
+            nc.sync.dma_start(w2_raw[:, t, :], w2_rows[t])
+        nc.sync.dma_start(gate_last[:], gate_rows[:, :, 2 * P :])
         nc.sync.dma_start(gate2_sb[:], gate2.rearrange("d p r -> p d r"))
         nc.sync.dma_start(nxt_sb[1][:], nxt2)
-        nc.sync.dma_start(nxt_sb[0][:], nxt1)
         make_identity(nc, ident[:])
-        warm = held([P, 8], F32, "warm")
-        nc.vector.memset(warm[:, :1], 0.0)
-        nc.scalar.activation(warm[:, 4:5], warm[:, :1], ACT.Gelu_apprx_tanh)
 
         def quantise(grouped, width, name):
             codes = held([P, width], U32, name + "_codes")
@@ -78,10 +77,10 @@ def tile_picked_hop2_gelu_p_kernel(
         w1_first = ring.tile([P, 4 * P], BF16, name="w1_first", tag="first", bufs=1, align_bytes=64)
         w1_rest = held([P, 3 * 4 * P], BF16, "w1_rest")
         for i in range(2):
-            raw = w1_raw[i][:].rearrange("p j (m t) -> p m j t", t=4)
-            nc.scalar.copy(w1_first[:].rearrange("p (m j) -> p m j", j=4)[:, :, 2 * i : 2 * i + 2], raw[:, :, :, 0])
+            raw = w1_raw[i][:].rearrange("p j (b t r) -> p t b r j", t=4, r=8)
+            nc.scalar.copy(w1_first[:].rearrange("p (b r j) -> p b r j", r=8, j=4)[:, 8 * i : 8 * (i + 1)], raw[:, 0])
             nc.scalar.copy(
-                w1_rest[:].rearrange("p (t m j) -> p m j t", t=3, j=4)[:, :, 2 * i : 2 * i + 2, :], raw[:, :, :, 1:]
+                w1_rest[:].rearrange("p (t b r j) -> p t b r j", t=3, r=8, j=4)[:, :, 8 * i : 8 * (i + 1)], raw[:, 1:]
             )
 
         x_codes, x_exps = [], []
@@ -100,7 +99,7 @@ def tile_picked_hop2_gelu_p_kernel(
             w1_q.append(quantise(w1_rest[:, 4 * P * (t - 1) : 4 * P * t], P, "w1_%d" % t))
 
         def bank(shape):
-            return psum.tile(shape, F32, name="bank", tag="bank", bufs=5)
+            return psum.tile(shape, F32, name="bank", tag="bank", bufs=6)
 
         h = []
         for t in range(4):
@@ -128,8 +127,8 @@ def tile_picked_hop2_gelu_p_kernel(
         )
         w2_codes, w2_scales = quantise(w2_grouped[:].rearrange("p n j -> p (n j)"), N, "w2")
 
-        z_sum = [psum.tile([P, H], F32, name="z_sum%d" % b) for b in range(3)]
-        z_rows = [held([P, 2, P, 2], BF16, "z_rows%d" % b) for b in range(3)]
+        z_sum = [psum.tile([P, H], F32, name="z_sum%d" % b) for b in range(2)]
+        z_rows = [held([P, 2, P, 2], BF16, "z_rows%d" % b) for b in range(2)]
 
         def gather(dst, t, d, v0, width, weights):
             nc.vector.tensor_tensor(dst, h[t][:].indirect(pos_sb[d][:, v0 // 16 : (v0 + width) // 16]), weights, MULT)
@@ -184,30 +183,29 @@ def tile_picked_hop2_gelu_p_kernel(
                 )
                 nc.scalar.activation(g[m][:, v0 : v0 + width], acc[:], ACT.Relu)
 
-        for t in range(2):
-            gather_and_turn(t, 0, 3 * P)
-        for b in range(3):
-            round_rows(b, 0)
-        gather_and_turn(2, 0, 3 * P)
-        gather_and_turn(3, 0, 2 * P)
-        gather_and_turn(3, 2 * P, P)
-        last = ring.tile([P, 10 * P], F32, name="last", tag="last", bufs=1, align_bytes=64)
-        for b in range(3):
-            round_rows(b, 1)
-        grouped = last[:, 6 * P :].bitcast(BF16)
+        for t in range(4):
+            gather_and_turn(t, 0, 2 * P)
+            if t % 2 == 1:
+                for b in range(2):
+                    round_rows(b, t // 2)
+        last = ring.tile([P, 16 * P], F32, name="last", tag="last", bufs=1, align_bytes=64)
+        grouped = last[:, 12 * P :].bitcast(BF16)
         turn_back([0, 1], grouped)
         second_layer(grouped, 0, 2 * P)
-        for t in range(4):
+        for t in range(3):
             for d in range(2):
-                c0 = (2 * t + d) * P
-                gather(last[:, c0 : c0 + P], t, d, 3 * P, P, gate_last[:, d, :])
-        grouped = ring.tile([P, 4 * P], BF16, name="grouped", tag="grouped", bufs=1, align_bytes=64)
-        turn_back([2], grouped[:])
-        second_layer(grouped[:], 2 * P, P)
-        grouped = ring.tile([P, 4 * P], BF16, name="grouped", tag="grouped", bufs=1, align_bytes=64)
-        terms = last[:, : 8 * P].rearrange("p (t d c i) -> p d c t i", t=4, d=2, i=4)
-        nc.vector.tensor_tensor(grouped[:].rearrange("p (c i t) -> p c t i", i=4, t=4), terms[:, 0], terms[:, 1], ADD)
-        second_layer(grouped[:], 3 * P, P)
+                c0 = (2 * t + d) * 2 * P
+                gather(last[:, c0 : c0 + 2 * P], t, d, 2 * P, 2 * P, gate_last[:, d, :])
+        for b in range(2):
+            for d in range(2):
+                c0 = (6 + d) * 2 * P + b * P
+                gather(last[:, c0 : c0 + P], 3, d, (2 + b) * P, P, gate_last[:, d, b * P : (b + 1) * P])
+            grouped = held([P, 4 * P], BF16, "grouped%d" % b)
+            both = last[:].rearrange("p (t d b c i) -> p d b c t i", t=4, d=2, b=2, i=4)
+            nc.vector.tensor_tensor(
+                grouped[:].rearrange("p (c i t) -> p c t i", i=4, t=4), both[:, 0, b], both[:, 1, b], ADD
+            )
+            second_layer(grouped[:], (2 + b) * P, P)
 
         terms = []
         for m in range(2):

@@ -19,7 +19,13 @@ MULT = mybir.AluOpType.mult
 ADD = mybir.AluOpType.add
 
 P = 128
-HALF = 512
+PACK = 4
+LIST_ROWS = 16
+HALF = S // 2
+V_HALF = V // 2
+WORD_LOADS = 4
+CLEAR_ON_VECTOR = 640
+RING_BANKS = 6
 
 
 def tile_picked_hop2_gelu_p_kernel(
@@ -28,45 +34,20 @@ def tile_picked_hop2_gelu_p_kernel(
     nc = tc.nc
     with ExitStack() as ctx:
         keep = ctx.enter_context(tc.tile_pool(name="keep", bufs=1))
-        ring = ctx.enter_context(tc.tile_pool(name="ring", bufs=1))
+        shared = ctx.enter_context(tc.tile_pool(name="shared", bufs=1))
         psum = ctx.enter_context(tc.psum_pool(name="psum", bufs=1))
 
         def held(shape, dtype, name):
             return keep.tile(shape, dtype, name=name, align_bytes=64)
 
-        offs_sb = held([P, S // 16], U16, "offs_sb")
-        pos_sb = [held([P, V // 16], U16, "pos%d" % d) for d in range(2)]
-        nxt_sb = [held([P, U // 16], U16, "nxt%d" % d) for d in range(2)]
-        words_all = held([P, T], U16, "words_all")
-        scales_all = held([P, T], U8, "scales_all")
-        w1_raw = [held([P, 4, H // 2], F32, "w1_raw%d" % i) for i in range(2)]
-        w2_raw = held([P, 4, N], F32, "w2_raw")
-        gate_main = ring.tile([P, 2, 2 * P], F32, name="gate_main", tag="last", bufs=1, align_bytes=64)
-        gate_last = held([P, 2, 2 * P], F32, "gate_last")
-        gate2_sb = held([P, 2, U], F32, "gate2_sb")
-        ident = held([P, P], F32, "ident")
+        def in_slot(slot, shape, dtype, name):
+            return shared.tile(shape, dtype, name=name, tag=slot, bufs=1, align_bytes=64)
 
-        nc.vector.memset(scales_all[:].bitcast(I32), 0)
-        w1_rows = w1.rearrange("(p j) n -> p j n", j=4)
-        nc.sync.dma_start(offs_sb[:], offs)
-        nc.sync.dma_start(words_all[:].bitcast(I32), x_words[0].bitcast(I32))
-        nc.sync.dma_start(pos_sb[0][:], pos1)
-        nc.sync.dma_start(pos_sb[1][:], pos2)
-        nc.sync.dma_start(w1_raw[0][:], w1_rows[:, :, :256])
-        scale_words = x_scales[0].bitcast(I32)
-        for q in range(4):
-            nc.sync.dma_start(scales_all[32 * q : 32 * q + 4, :].bitcast(I32), scale_words[4 * q : 4 * q + 4, :])
-        nc.sync.dma_start(nxt_sb[0][:], nxt1)
-        nc.sync.dma_start(w1_raw[1][:], w1_rows[:, :, 256:])
-        gate_rows = gate.rearrange("d p v -> p d v")
-        nc.sync.dma_start(gate_main[:], gate_rows[:, :, : 2 * P])
-        w2_rows = w2.rearrange("(b t r) n -> t b r n", t=4, r=8)
-        for t in range(4):
-            nc.sync.dma_start(w2_raw[:, t, :], w2_rows[t])
-        nc.sync.dma_start(gate_last[:], gate_rows[:, :, 2 * P :])
-        nc.sync.dma_start(gate2_sb[:], gate2.rearrange("d p r -> p d r"))
-        nc.sync.dma_start(nxt_sb[1][:], nxt2)
-        make_identity(nc, ident[:])
+        def bank(shape):
+            return psum.tile(shape, F32, name="bank", tag="bank", bufs=RING_BANKS)
+
+        def entries(list_tile, first, count):
+            return list_tile[:, first // LIST_ROWS : (first + count) // LIST_ROWS]
 
         def quantise(grouped, width, name):
             codes = held([P, width], U32, name + "_codes")
@@ -74,38 +55,75 @@ def tile_picked_hop2_gelu_p_kernel(
             nc.vector.quantize_mx(out=codes[:].bitcast(FP8X4), scales=scales[:], in_=grouped)
             return codes, scales
 
-        w1_first = ring.tile([P, 4 * P], BF16, name="w1_first", tag="first", bufs=1, align_bytes=64)
-        w1_rest = held([P, 3 * 4 * P], BF16, "w1_rest")
+        offs_sb = held([P, S // LIST_ROWS], U16, "offs_sb")
+        pos_sb = [held([P, V // LIST_ROWS], U16, "pos%d" % d) for d in range(2)]
+        nxt_sb = [held([P, U // LIST_ROWS], U16, "nxt%d" % d) for d in range(2)]
+        words_all = held([P, T], U16, "words_all")
+        scales_all = held([P, T], U8, "scales_all")
+        w1_raw = [held([P, PACK, H // 2], F32, "w1_raw%d" % i) for i in range(2)]
+        w2_raw = held([P, PACK, N], F32, "w2_raw")
+        gate_turned = in_slot("late_terms", [P, 2, V_HALF], F32, "gate_turned")
+        gate_direct = held([P, 2, V_HALF], F32, "gate_direct")
+        gate2_sb = held([P, 2, U], F32, "gate2_sb")
+        ident = held([P, P], F32, "ident")
+
+        nc.vector.memset(scales_all[:].bitcast(I32)[:, :CLEAR_ON_VECTOR], 0)
+        nc.gpsimd.memset(scales_all[:].bitcast(I32)[:, CLEAR_ON_VECTOR:], 0)
+        piece = T // 2 // WORD_LOADS
+        for i in range(WORD_LOADS):
+            cols = slice(piece * i, piece * (i + 1))
+            nc.sync.dma_start(words_all[:].bitcast(I32)[:, cols], x_words[0].bitcast(I32)[:, cols])
+        nc.sync.dma_start(offs_sb[:], offs)
+        scale_rows = x_scales[0].bitcast(I32)
+        for q in range(4):
+            nc.sync.dma_start(scales_all[32 * q : 32 * q + 4, :].bitcast(I32), scale_rows[4 * q : 4 * q + 4, :])
+        w1_rows = w1.rearrange("(p j) n -> p j n", j=PACK)
         for i in range(2):
-            raw = w1_raw[i][:].rearrange("p j (b t r) -> p t b r j", t=4, r=8)
-            nc.scalar.copy(w1_first[:].rearrange("p (b r j) -> p b r j", r=8, j=4)[:, 8 * i : 8 * (i + 1)], raw[:, 0])
+            nc.sync.dma_start(w1_raw[i][:], w1_rows[:, :, H // 2 * i : H // 2 * (i + 1)])
+        nc.sync.dma_start(pos_sb[0][:], pos1)
+        nc.sync.dma_start(pos_sb[1][:], pos2)
+        gate_rows = gate.rearrange("d p v -> p d v")
+        nc.sync.dma_start(gate_turned[:], gate_rows[:, :, :V_HALF])
+        w2_rows = w2.rearrange("(q t r) n -> t q r n", t=PACK, r=8)
+        for t in range(PACK):
+            nc.sync.dma_start(w2_raw[:, t, :], w2_rows[t])
+        nc.sync.dma_start(gate_direct[:], gate_rows[:, :, V_HALF:])
+        nc.sync.dma_start(gate2_sb[:], gate2.rearrange("d p r -> p d r"))
+        nc.sync.dma_start(nxt_sb[1][:], nxt2)
+        nc.sync.dma_start(nxt_sb[0][:], nxt1)
+        make_identity(nc, ident[:])
+
+        w1_first = in_slot("last_exps", [P, PACK * P], BF16, "w1_first")
+        w1_rest = held([P, (PACK - 1) * PACK * P], BF16, "w1_rest")
+        for i in range(2):
+            blocks = slice(8 * i, 8 * (i + 1))
+            raw = w1_raw[i][:].rearrange("p j (q t r) -> p t q r j", t=PACK, r=8)
+            nc.scalar.copy(w1_first[:].rearrange("p (q r j) -> p q r j", r=8, j=PACK)[:, blocks], raw[:, 0])
             nc.scalar.copy(
-                w1_rest[:].rearrange("p (t b r j) -> p t b r j", t=3, r=8, j=4)[:, :, 8 * i : 8 * (i + 1)], raw[:, 1:]
+                w1_rest[:].rearrange("p (t q r j) -> p t q r j", t=PACK - 1, r=8, j=PACK)[:, :, blocks], raw[:, 1:]
             )
 
         x_codes, x_exps = [], []
         for half in range(2):
             codes = held([P, HALF], U16, "x_codes%d" % half)
-            nc.vector.tensor_copy(codes[:], words_all[:].indirect(offs_sb[:, 32 * half : 32 * half + 32]))
+            nc.vector.tensor_copy(codes[:], words_all[:].indirect(entries(offs_sb, HALF * half, HALF)))
             x_codes.append(codes)
-        exps = held([P, HALF], U8, "x_exps0")
-        nc.vector.tensor_copy(exps[:], scales_all[:].indirect(offs_sb[:, :32]))
-        x_exps.append(exps)
+        x_exps.append(held([P, HALF], U8, "x_exps0"))
+        nc.vector.tensor_copy(x_exps[0][:], scales_all[:].indirect(entries(offs_sb, 0, HALF)))
         w1_q = [quantise(w1_first[:], P, "w1_0")]
-        exps = ring.tile([P, HALF], U8, name="x_exps1", tag="first", bufs=1, align_bytes=64)
-        nc.vector.tensor_copy(exps[:], scales_all[:].indirect(offs_sb[:, 32:]))
-        x_exps.append(exps)
-        for t in range(1, 4):
-            w1_q.append(quantise(w1_rest[:, 4 * P * (t - 1) : 4 * P * t], P, "w1_%d" % t))
-
-        def bank(shape):
-            return psum.tile(shape, F32, name="bank", tag="bank", bufs=6)
+        x_exps.append(in_slot("last_exps", [P, HALF], U8, "x_exps1"))
+        nc.vector.tensor_copy(x_exps[1][:], scales_all[:].indirect(entries(offs_sb, HALF, HALF)))
+        for t in range(1, PACK):
+            w1_q.append(quantise(w1_rest[:, PACK * P * (t - 1) : PACK * P * t], P, "w1_%d" % t))
 
         h = []
-        for t in range(4):
+        for t in range(PACK):
             h_t = held([P, S], F32, "h%d" % t)
             codes, scales = w1_q[t]
-            pieces = [(0, 512), (512, 256), (768, 256)] if t == 0 else [(0, 512), (512, 512)]
+            if t == 0:
+                pieces = [(0, HALF), (HALF, HALF // 2), (HALF + HALF // 2, HALF // 2)]
+            else:
+                pieces = [(0, HALF), (HALF, HALF)]
             for c0, width in pieces:
                 acc = bank([P, width])
                 cols = slice(c0 % HALF, c0 % HALF + width)
@@ -121,50 +139,14 @@ def tile_picked_hop2_gelu_p_kernel(
                 nc.scalar.activation(h_t[:, c0 : c0 + width], acc[:], ACT.Gelu_apprx_tanh)
             h.append(h_t)
 
-        w2_grouped = held([P, N, 4], BF16, "w2_grouped")
+        w2_grouped = held([P, N, PACK], BF16, "w2_grouped")
         nc.vector.tensor_copy(
-            w2_grouped[:].rearrange("p (c i) j -> p c j i", i=4), w2_raw[:].rearrange("p j (c i) -> p c j i", i=4)
+            w2_grouped[:].rearrange("p (c n) t -> p c t n", n=4), w2_raw[:].rearrange("p t (c n) -> p c t n", n=4)
         )
-        w2_codes, w2_scales = quantise(w2_grouped[:].rearrange("p n j -> p (n j)"), N, "w2")
+        w2_codes, w2_scales = quantise(w2_grouped[:].rearrange("p n t -> p (n t)"), N, "w2")
 
-        z_sum = [psum.tile([P, H], F32, name="z_sum%d" % b) for b in range(2)]
-        z_rows = [held([P, 2, P, 2], BF16, "z_rows%d" % b) for b in range(2)]
-
-        def gather(dst, t, d, v0, width, weights):
-            nc.vector.tensor_tensor(dst, h[t][:].indirect(pos_sb[d][:, v0 // 16 : (v0 + width) // 16]), weights, MULT)
-
-        def gather_and_turn(t, v0, width):
-            parts = []
-            for d in range(2):
-                part = held([P, width], F32, "part%d_%d_%d" % (t, v0, d))
-                gather(part[:], t, d, v0, width, gate_main[:, d, v0 : v0 + width])
-                parts.append(part)
-            for b in range(v0 // P, (v0 + width) // P):
-                for d in range(2):
-                    nc.tensor.matmul(
-                        z_sum[b][:, P * t : P * (t + 1)],
-                        parts[d][:, P * b - v0 : P * (b + 1) - v0],
-                        ident[:],
-                        start=(d == 0),
-                        stop=(d == 1),
-                        is_transpose=True,
-                    )
-
-        def round_rows(b, u):
-            nc.scalar.copy(
-                z_rows[b][:, u, :, :], z_sum[b][:, 2 * P * u : 2 * P * (u + 1)].rearrange("v (e p) -> v p e", e=2)
-            )
-
-        def turn_back(blocks, grouped):
-            turned = bank([P, len(blocks), 2, P])
-            for i, b in enumerate(blocks):
-                pairs = z_rows[b][:].rearrange("v u p e -> v (u p e)").bitcast(F32)
-                for u in range(2):
-                    nc.tensor.transpose(turned[:, i, u, :], pairs[:, P * u : P * (u + 1)], ident[:])
-            nc.scalar.copy(
-                grouped.bitcast(F32).rearrange("p (b v u) -> p b v u", v=P, u=2),
-                turned[:].rearrange("p b u v -> p b v u"),
-            )
+        def weighted_gather(dst, t, d, v0, width, weights):
+            nc.vector.tensor_tensor(dst, h[t][:].indirect(entries(pos_sb[d], v0, width)), weights, MULT)
 
         g = [held([P, V], F32, "g%d" % m) for m in range(2)]
 
@@ -183,37 +165,69 @@ def tile_picked_hop2_gelu_p_kernel(
                 )
                 nc.scalar.activation(g[m][:, v0 : v0 + width], acc[:], ACT.Relu)
 
-        for t in range(4):
-            gather_and_turn(t, 0, 2 * P)
-            if t % 2 == 1:
-                for b in range(2):
-                    round_rows(b, t // 2)
-        last = ring.tile([P, 16 * P], F32, name="last", tag="last", bufs=1, align_bytes=64)
-        grouped = last[:, 12 * P :].bitcast(BF16)
-        turn_back([0, 1], grouped)
-        second_layer(grouped, 0, 2 * P)
-        for t in range(3):
+        z_sum = [psum.tile([P, H], F32, name="z_sum%d" % b) for b in range(2)]
+        z_rows = [held([P, 2, P, 2], BF16, "z_rows%d" % b) for b in range(2)]
+        for t in range(PACK):
+            parts = []
             for d in range(2):
-                c0 = (2 * t + d) * 2 * P
-                gather(last[:, c0 : c0 + 2 * P], t, d, 2 * P, 2 * P, gate_last[:, d, :])
+                part = held([P, V_HALF], F32, "part%d_%d" % (t, d))
+                weighted_gather(part[:], t, d, 0, V_HALF, gate_turned[:, d, :])
+                parts.append(part)
+            for b in range(2):
+                for d in range(2):
+                    nc.tensor.matmul(
+                        z_sum[b][:, P * t : P * (t + 1)],
+                        parts[d][:, P * b : P * (b + 1)],
+                        ident[:],
+                        start=(d == 0),
+                        stop=(d == 1),
+                        is_transpose=True,
+                    )
+            if t % 2 == 1:
+                u = t // 2
+                for b in range(2):
+                    nc.scalar.copy(
+                        z_rows[b][:, u, :, :],
+                        z_sum[b][:, 2 * P * u : 2 * P * (u + 1)].rearrange("v (e p) -> v p e", e=2),
+                    )
+
+        late = in_slot("late_terms", [P, PACK * 2 * V_HALF], F32, "late")
+        early_grouped = late[:, (PACK - 1) * 2 * V_HALF :].bitcast(BF16)
+        turned = bank([P, 2, 2, P])
+        for b in range(2):
+            pairs = z_rows[b][:].rearrange("v u p e -> v (u p e)").bitcast(F32)
+            for u in range(2):
+                nc.tensor.transpose(turned[:, b, u, :], pairs[:, P * u : P * (u + 1)], ident[:])
+        nc.scalar.copy(
+            early_grouped.bitcast(F32).rearrange("p (b v u) -> p b v u", v=P, u=2),
+            turned[:].rearrange("p b u v -> p b v u"),
+        )
+        second_layer(early_grouped, 0, V_HALF)
+
+        for t in range(PACK - 1):
+            for d in range(2):
+                c0 = (2 * t + d) * V_HALF
+                weighted_gather(late[:, c0 : c0 + V_HALF], t, d, V_HALF, V_HALF, gate_direct[:, d, :])
+        terms = late[:].rearrange("p (t d b c v) -> p d b c t v", t=PACK, d=2, b=2, v=4)
         for b in range(2):
             for d in range(2):
-                c0 = (6 + d) * 2 * P + b * P
-                gather(last[:, c0 : c0 + P], 3, d, (2 + b) * P, P, gate_last[:, d, b * P : (b + 1) * P])
-            grouped = held([P, 4 * P], BF16, "grouped%d" % b)
-            both = last[:].rearrange("p (t d b c i) -> p d b c t i", t=4, d=2, b=2, i=4)
+                c0 = (2 * (PACK - 1) + d) * V_HALF + b * P
+                weighted_gather(
+                    late[:, c0 : c0 + P], PACK - 1, d, V_HALF + b * P, P, gate_direct[:, d, b * P : (b + 1) * P]
+                )
+            grouped = held([P, PACK * P], BF16, "late_grouped%d" % b)
             nc.vector.tensor_tensor(
-                grouped[:].rearrange("p (c i t) -> p c t i", i=4, t=4), both[:, 0, b], both[:, 1, b], ADD
+                grouped[:].rearrange("p (c v t) -> p c t v", v=4, t=PACK), terms[:, 0, b], terms[:, 1, b], ADD
             )
-            second_layer(grouped[:], (2 + b) * P, P)
+            second_layer(grouped[:], V_HALF + b * P, P)
 
-        terms = []
+        roots = []
         for m in range(2):
             for d in range(2):
-                term = held([P, U], F32, "term%d%d" % (m, d))
-                nc.vector.tensor_tensor(term[:], g[m][:].indirect(nxt_sb[d][:]), gate2_sb[:, d, :], MULT)
-                terms.append(term)
+                root = held([P, U], F32, "root%d%d" % (m, d))
+                nc.vector.tensor_tensor(root[:], g[m][:].indirect(nxt_sb[d][:]), gate2_sb[:, d, :], MULT)
+                roots.append(root)
         for m in range(2):
             result = held([P, U], F32, "result%d" % m)
-            nc.vector.tensor_tensor(result[:], terms[2 * m][:], terms[2 * m + 1][:], ADD)
+            nc.vector.tensor_tensor(result[:], roots[2 * m][:], roots[2 * m + 1][:], ADD)
             nc.sync.dma_start(out[P * m : P * (m + 1), :], result[:])

@@ -23,8 +23,8 @@ PACK = 4
 LIST_ROWS = 16
 HALF = S // 2
 V_HALF = V // 2
-WORD_LOADS = 4
 CLEAR_ON_VECTOR = 640
+W1_FRONT = 128
 RING_BANKS = 6
 
 
@@ -58,70 +58,78 @@ def tile_picked_hop2_gelu_p_kernel(
         offs_sb = held([P, S // LIST_ROWS], U16, "offs_sb")
         pos_sb = [held([P, V // LIST_ROWS], U16, "pos%d" % d) for d in range(2)]
         nxt_sb = [held([P, U // LIST_ROWS], U16, "nxt%d" % d) for d in range(2)]
-        words_all = held([P, T], U16, "words_all")
-        scales_all = held([P, T], U8, "scales_all")
-        w1_raw = [held([P, PACK, H // 2], F32, "w1_raw%d" % i) for i in range(2)]
-        w2_raw = held([P, PACK, N], F32, "w2_raw")
-        gate_turned = in_slot("late_terms", [P, 2, V_HALF], F32, "gate_turned")
-        gate_direct = held([P, 2, V_HALF], F32, "gate_direct")
-        gate2_sb = held([P, 2, U], F32, "gate2_sb")
+        words_all = in_slot("late_gates", [P, T], U16, "words_all")
+        scales_all = in_slot("late_terms", [P, T], U8, "scales_all")
+        x_exps = held([P, S], U8, "x_exps")
+        w1_cuts = [0, W1_FRONT, H]
+        w1_raw = [held([P, PACK, w1_cuts[i + 1] - w1_cuts[i]], F32, "w1_raw%d" % i) for i in range(2)]
         ident = held([P, P], F32, "ident")
 
         nc.vector.memset(scales_all[:].bitcast(I32)[:, :CLEAR_ON_VECTOR], 0)
         nc.gpsimd.memset(scales_all[:].bitcast(I32)[:, CLEAR_ON_VECTOR:], 0)
-        piece = T // 2 // WORD_LOADS
-        for i in range(WORD_LOADS):
-            cols = slice(piece * i, piece * (i + 1))
-            nc.sync.dma_start(words_all[:].bitcast(I32)[:, cols], x_words[0].bitcast(I32)[:, cols])
-        nc.sync.dma_start(offs_sb[:], offs)
-        scale_rows = x_scales[0].bitcast(I32)
-        for q in range(4):
-            nc.sync.dma_start(scales_all[32 * q : 32 * q + 4, :].bitcast(I32), scale_rows[4 * q : 4 * q + 4, :])
+        nc.vector.memset(x_exps[:].bitcast(I32), 0)
         w1_rows = w1.rearrange("(p j) n -> p j n", j=PACK)
-        for i in range(2):
-            nc.sync.dma_start(w1_raw[i][:], w1_rows[:, :, H // 2 * i : H // 2 * (i + 1)])
+        nc.sync.dma_start(offs_sb[:], offs)
+        nc.sync.dma_start(w1_raw[0][:], w1_rows[:, :, :W1_FRONT])
         nc.sync.dma_start(pos_sb[0][:], pos1)
         nc.sync.dma_start(pos_sb[1][:], pos2)
+        nc.sync.dma_start(nxt_sb[0][:], nxt1)
+        nc.sync.dma_start(nxt_sb[1][:], nxt2)
+        nc.sync.dma_start(scales_all[:].bitcast(I32)[0:P:8, :], x_scales[0].bitcast(I32))
+        nc.sync.dma_start(words_all[:].bitcast(I32), x_words[0].bitcast(I32))
+        nc.sync.dma_start(w1_raw[1][:], w1_rows[:, :, W1_FRONT:])
+        make_identity(nc, ident[:])
+
+        spread_exps = held([P, S], U8, "spread_exps")
+        nc.vector.tensor_copy(spread_exps[:], scales_all[:].indirect(offs_sb[:]))
+        for j in range(4):
+            nc.sync.dma_start(x_exps[:].bitcast(I32)[j:P:32, :], spread_exps[:].bitcast(I32)[8 * j : P : 32, :])
+
+        early_weights = in_slot("late_terms", [P, 2 * V_HALF + PACK * N], F32, "early_weights")
+        gate_turned = early_weights[:, : 2 * V_HALF].rearrange("p (d v) -> p d v", d=2)
+        w2_raw = early_weights[:, 2 * V_HALF :].rearrange("p (t n) -> p t n", t=PACK)
         gate_rows = gate.rearrange("d p v -> p d v")
-        nc.sync.dma_start(gate_turned[:], gate_rows[:, :, :V_HALF])
         w2_rows = w2.rearrange("(q t r) n -> t q r n", t=PACK, r=8)
         for t in range(PACK):
             nc.sync.dma_start(w2_raw[:, t, :], w2_rows[t])
-        nc.sync.dma_start(gate_direct[:], gate_rows[:, :, V_HALF:])
-        nc.sync.dma_start(gate2_sb[:], gate2.rearrange("d p r -> p d r"))
-        nc.sync.dma_start(nxt_sb[1][:], nxt2)
-        nc.sync.dma_start(nxt_sb[0][:], nxt1)
-        make_identity(nc, ident[:])
+        nc.sync.dma_start(gate_turned, gate_rows[:, :, :V_HALF])
 
-        w1_first = in_slot("last_exps", [P, PACK * P], BF16, "w1_first")
-        w1_rest = held([P, (PACK - 1) * PACK * P], BF16, "w1_rest")
-        for i in range(2):
-            blocks = slice(8 * i, 8 * (i + 1))
-            raw = w1_raw[i][:].rearrange("p j (q t r) -> p t q r j", t=PACK, r=8)
-            nc.scalar.copy(w1_first[:].rearrange("p (q r j) -> p q r j", r=8, j=PACK)[:, blocks], raw[:, 0])
-            nc.scalar.copy(
-                w1_rest[:].rearrange("p (t q r j) -> p t q r j", t=PACK - 1, r=8, j=PACK)[:, :, blocks], raw[:, 1:]
-            )
+        front = W1_FRONT
+        staged = [held([P, front + PACK * P + PACK * N], BF16, "staged0"), held([P, front + PACK * P], BF16, "staged1")]
+        w1_grouped = [staged[t % 2][:, front * (1 - t // 2) :][:, : PACK * P] for t in range(PACK)]
 
-        x_codes, x_exps = [], []
+        def round_w1(copy, t, i):
+            raw = w1_raw[i][:].rearrange("p j (q t c n) -> p t q c j n", t=PACK, c=2, n=4)
+            dst = w1_grouped[t].rearrange("p (q c n j) -> p q c j n", c=2, n=4, j=PACK)
+            copy(dst[:, w1_cuts[i] // 32 : w1_cuts[i + 1] // 32], raw[:, t])
+
+        for t in range(PACK):
+            round_w1(nc.scalar.copy, t, 0)
+        for t in range(2):
+            round_w1(nc.scalar.copy, t, 1)
+
+        x_codes = []
         for half in range(2):
             codes = held([P, HALF], U16, "x_codes%d" % half)
             nc.vector.tensor_copy(codes[:], words_all[:].indirect(entries(offs_sb, HALF * half, HALF)))
             x_codes.append(codes)
-        x_exps.append(held([P, HALF], U8, "x_exps0"))
-        nc.vector.tensor_copy(x_exps[0][:], scales_all[:].indirect(entries(offs_sb, 0, HALF)))
-        w1_q = [quantise(w1_first[:], P, "w1_0")]
-        x_exps.append(in_slot("last_exps", [P, HALF], U8, "x_exps1"))
-        nc.vector.tensor_copy(x_exps[1][:], scales_all[:].indirect(entries(offs_sb, HALF, HALF)))
-        for t in range(1, PACK):
-            w1_q.append(quantise(w1_rest[:, PACK * P * (t - 1) : PACK * P * t], P, "w1_%d" % t))
+        w1_q = [quantise(w1_grouped[t], P, "w1_%d" % t) for t in range(2)]
+        for t in range(2, PACK):
+            round_w1(nc.vector.tensor_copy, t, 1)
+        w1_q.extend(quantise(w1_grouped[t], P, "w1_%d" % t) for t in range(2, PACK))
+
+        late_gates = in_slot("late_gates", [P, 2 * V_HALF + 2 * U], F32, "late_gates")
+        gate_direct = late_gates[:, : 2 * V_HALF].rearrange("p (d v) -> p d v", d=2)
+        gate2_sb = late_gates[:, 2 * V_HALF :].rearrange("p (d r) -> p d r", d=2)
+        nc.sync.dma_start(gate_direct, gate_rows[:, :, V_HALF:])
+        nc.sync.dma_start(gate2_sb, gate2.rearrange("d p r -> p d r"))
 
         h = []
         for t in range(PACK):
             h_t = held([P, S], F32, "h%d" % t)
             codes, scales = w1_q[t]
             if t == 0:
-                pieces = [(0, HALF), (HALF, HALF // 2), (HALF + HALF // 2, HALF // 2)]
+                pieces = [(0, HALF // 2), (HALF // 2, HALF // 2), (HALF, HALF)]
             else:
                 pieces = [(0, HALF), (HALF, HALF)]
             for c0, width in pieces:
@@ -132,18 +140,18 @@ def tile_picked_hop2_gelu_p_kernel(
                     lhsT=codes[:].bitcast(FP8X4),
                     lhsT_scale=scales[:],
                     rhs=x_codes[c0 // HALF][:, cols].bitcast(FP4X4),
-                    rhs_scale=x_exps[c0 // HALF][:, cols],
+                    rhs_scale=x_exps[:, c0 : c0 + width],
                     start=True,
                     stop=True,
                 )
                 nc.scalar.activation(h_t[:, c0 : c0 + width], acc[:], ACT.Gelu_apprx_tanh)
             h.append(h_t)
 
-        w2_grouped = held([P, N, PACK], BF16, "w2_grouped")
+        w2_grouped = staged[0][:, PACK * P : PACK * (P + N)]
         nc.vector.tensor_copy(
-            w2_grouped[:].rearrange("p (c n) t -> p c t n", n=4), w2_raw[:].rearrange("p t (c n) -> p c t n", n=4)
+            w2_grouped.rearrange("p (c n t) -> p c t n", n=4, t=PACK), w2_raw.rearrange("p t (c n) -> p c t n", n=4)
         )
-        w2_codes, w2_scales = quantise(w2_grouped[:].rearrange("p n t -> p (n t)"), N, "w2")
+        w2_codes, w2_scales = quantise(w2_grouped, N, "w2")
 
         def weighted_gather(dst, t, d, v0, width, weights):
             nc.vector.tensor_tensor(dst, h[t][:].indirect(entries(pos_sb[d], v0, width)), weights, MULT)

@@ -25,6 +25,9 @@ HALF = S // 2
 V_HALF = V // 2
 CLEAR_ON_VECTOR = 640
 W1_FRONT = 128
+LATE_GROUPS = (128, 64, 64)
+LATE_PITCH = 1216
+OVERLAP = (128, 64)
 RING_BANKS = 6
 
 
@@ -85,23 +88,25 @@ def tile_picked_hop2_gelu_p_kernel(
         for j in range(4):
             nc.sync.dma_start(x_exps[:].bitcast(I32)[j:P:32, :], spread_exps[:].bitcast(I32)[8 * j : P : 32, :])
 
-        early_weights = in_slot("late_terms", [P, 2 * V_HALF + PACK * N], F32, "early_weights")
-        gate_turned = early_weights[:, : 2 * V_HALF].rearrange("p (d v) -> p d v", d=2)
-        w2_raw = early_weights[:, 2 * V_HALF :].rearrange("p (t n) -> p t n", t=PACK)
+        stage = in_slot("late_terms", [P, 2 * LATE_PITCH + PACK * N], F32, "stage")
+        late = [stage[:, LATE_PITCH * d : LATE_PITCH * d + PACK * V_HALF] for d in range(2)]
+        gate_turned = [late[d][:, 3 * P : 3 * P + V_HALF] for d in range(2)]
+        w2_raw = stage[:, 2 * LATE_PITCH :].rearrange("p (t n) -> p t n", t=PACK)
         gate_rows = gate.rearrange("d p v -> p d v")
-        w2_rows = w2.rearrange("(q t r) n -> t q r n", t=PACK, r=8)
-        for t in range(PACK):
-            nc.sync.dma_start(w2_raw[:, t, :], w2_rows[t])
-        nc.sync.dma_start(gate_turned, gate_rows[:, :, :V_HALF])
+        w2_rows = w2.rearrange("(q u r e) n -> u q r (e n)", u=2, r=8, e=2)
+        for u in range(2):
+            nc.sync.dma_start(stage[:, 2 * LATE_PITCH + 2 * N * u :][:, : 2 * N], w2_rows[u])
+        both_late = stage[:, : 2 * LATE_PITCH].rearrange("p (d c) -> p d c", d=2)
+        nc.sync.dma_start(both_late[:, :, 3 * P : 3 * P + V_HALF], gate_rows[:, :, :V_HALF])
 
         front = W1_FRONT
         staged = [held([P, front + PACK * P + PACK * N], BF16, "staged0"), held([P, front + PACK * P], BF16, "staged1")]
         w1_grouped = [staged[t % 2][:, front * (1 - t // 2) :][:, : PACK * P] for t in range(PACK)]
 
         def round_w1(copy, t, i):
-            raw = w1_raw[i][:].rearrange("p j (q t c n) -> p t q c j n", t=PACK, c=2, n=4)
-            dst = w1_grouped[t].rearrange("p (q c n j) -> p q c j n", c=2, n=4, j=PACK)
-            copy(dst[:, w1_cuts[i] // 32 : w1_cuts[i + 1] // 32], raw[:, t])
+            raw = w1_raw[i][:].rearrange("p j (q u c n e) -> p u e q c j n", u=2, c=4, n=2, e=2)
+            dst = w1_grouped[t].rearrange("p (q c n j) -> p q c j n", c=4, n=2, j=PACK)
+            copy(dst[:, w1_cuts[i] // 32 : w1_cuts[i + 1] // 32], raw[:, t // 2, t % 2])
 
         for t in range(PACK):
             round_w1(nc.scalar.copy, t, 0)
@@ -158,8 +163,7 @@ def tile_picked_hop2_gelu_p_kernel(
 
         g = [held([P, V], F32, "g%d" % m) for m in range(2)]
 
-        def second_layer(grouped, v0, width):
-            codes, scales = quantise(grouped, width, "z%d" % v0)
+        def second_layer(codes, scales, v0, width):
             for m in range(2):
                 acc = bank([P, width])
                 nc.tensor.matmul_mx(
@@ -179,7 +183,7 @@ def tile_picked_hop2_gelu_p_kernel(
             parts = []
             for d in range(2):
                 part = held([P, V_HALF], F32, "part%d_%d" % (t, d))
-                weighted_gather(part[:], t, d, 0, V_HALF, gate_turned[:, d, :])
+                weighted_gather(part[:], t, d, 0, V_HALF, gate_turned[d])
                 parts.append(part)
             for b in range(2):
                 for d in range(2):
@@ -199,35 +203,41 @@ def tile_picked_hop2_gelu_p_kernel(
                         z_sum[b][:, 2 * P * u : 2 * P * (u + 1)].rearrange("v (e p) -> v p e", e=2),
                     )
 
-        late = in_slot("late_terms", [P, PACK * 2 * V_HALF], F32, "late")
-        early_grouped = late[:, (PACK - 1) * 2 * V_HALF :].bitcast(BF16)
-        turned = bank([P, 2, 2, P])
+        early_codes = held([P, V_HALF], U32, "early_codes")
+        early_scales = held([P, V_HALF], U8, "early_scales")
         for b in range(2):
+            first = LATE_PITCH * b + PACK * V_HALF - OVERLAP[b]
+            words = stage[:, first : first + 2 * P]
+            turned = bank([P, 2, P])
             pairs = z_rows[b][:].rearrange("v u p e -> v (u p e)").bitcast(F32)
             for u in range(2):
-                nc.tensor.transpose(turned[:, b, u, :], pairs[:, P * u : P * (u + 1)], ident[:])
-        nc.scalar.copy(
-            early_grouped.bitcast(F32).rearrange("p (b v u) -> p b v u", v=P, u=2),
-            turned[:].rearrange("p b u v -> p b v u"),
-        )
-        second_layer(early_grouped, 0, V_HALF)
+                nc.tensor.transpose(turned[:, u, :], pairs[:, P * u : P * (u + 1)], ident[:])
+            nc.scalar.copy(words.rearrange("p (v u) -> p v u", u=2), turned[:].rearrange("p u v -> p v u"))
+            cols = slice(P * b, P * (b + 1))
+            nc.vector.quantize_mx(
+                out=early_codes[:, cols].bitcast(FP8X4), scales=early_scales[:, cols], in_=words.bitcast(BF16)
+            )
+        second_layer(early_codes, early_scales, 0, V_HALF)
 
         for t in range(PACK - 1):
             for d in range(2):
-                c0 = (2 * t + d) * V_HALF
-                weighted_gather(late[:, c0 : c0 + V_HALF], t, d, V_HALF, V_HALF, gate_direct[:, d, :])
-        terms = late[:].rearrange("p (t d b c v) -> p d b c t v", t=PACK, d=2, b=2, v=4)
-        for b in range(2):
+                weighted_gather(late[d][:, t * V_HALF : (t + 1) * V_HALF], t, d, V_HALF, V_HALF, gate_direct[:, d, :])
+        v0 = 0
+        for width in LATE_GROUPS:
+            cols = slice(v0, v0 + width)
+            terms = [late[d].rearrange("p (t v) -> p t v", t=PACK)[:, :, cols] for d in range(2)]
             for d in range(2):
-                c0 = (2 * (PACK - 1) + d) * V_HALF + b * P
-                weighted_gather(
-                    late[:, c0 : c0 + P], PACK - 1, d, V_HALF + b * P, P, gate_direct[:, d, b * P : (b + 1) * P]
-                )
-            grouped = held([P, PACK * P], BF16, "late_grouped%d" % b)
+                weighted_gather(terms[d][:, PACK - 1, :], PACK - 1, d, V_HALF + v0, width, gate_direct[:, d, cols])
+            grouped = held([P, PACK * width], BF16, "late_grouped%d" % v0)
             nc.vector.tensor_tensor(
-                grouped[:].rearrange("p (c v t) -> p c t v", v=4, t=PACK), terms[:, 0, b], terms[:, 1, b], ADD
+                grouped[:].rearrange("p (c v t) -> p c t v", v=4, t=PACK),
+                terms[0].rearrange("p t (c v) -> p c t v", v=4),
+                terms[1].rearrange("p t (c v) -> p c t v", v=4),
+                ADD,
             )
-            second_layer(grouped[:], V_HALF + b * P, P)
+            codes, scales = quantise(grouped[:], width, "z%d" % v0)
+            second_layer(codes, scales, V_HALF + v0, width)
+            v0 = v0 + width
 
         roots = []
         for m in range(2):

@@ -23,11 +23,8 @@ PACK = 4
 LIST_ROWS = 16
 HALF = S // 2
 V_HALF = V // 2
-CLEAR_ON_VECTOR = 640
-W1_FRONT = 128
-LATE_GROUPS = (128, 64, 64)
-LATE_PITCH = 1216
-OVERLAP = (128, 64)
+SCALE_ROW0 = P - 16
+W1_FRONT = 384
 RING_BANKS = 6
 
 
@@ -52,11 +49,8 @@ def tile_picked_hop2_gelu_p_kernel(
         def entries(list_tile, first, count):
             return list_tile[:, first // LIST_ROWS : (first + count) // LIST_ROWS]
 
-        def quantise(grouped, width, name):
-            codes = held([P, width], U32, name + "_codes")
-            scales = held([P, width], U8, name + "_scales")
-            nc.vector.quantize_mx(out=codes[:].bitcast(FP8X4), scales=scales[:], in_=grouped)
-            return codes, scales
+        def quantise(grouped, codes, scales):
+            nc.vector.quantize_mx(out=codes.bitcast(FP8X4), scales=scales, in_=grouped)
 
         offs_sb = held([P, S // LIST_ROWS], U16, "offs_sb")
         pos_sb = [held([P, V // LIST_ROWS], U16, "pos%d" % d) for d in range(2)]
@@ -68,60 +62,62 @@ def tile_picked_hop2_gelu_p_kernel(
         w1_raw = [held([P, PACK, w1_cuts[i + 1] - w1_cuts[i]], F32, "w1_raw%d" % i) for i in range(2)]
         ident = held([P, P], F32, "ident")
 
-        nc.vector.memset(scales_all[:].bitcast(I32)[:, :CLEAR_ON_VECTOR], 0)
-        nc.gpsimd.memset(scales_all[:].bitcast(I32)[:, CLEAR_ON_VECTOR:], 0)
+        nc.vector.memset(scales_all[:].bitcast(I32)[:SCALE_ROW0, :], 0)
         nc.vector.memset(x_exps[:].bitcast(I32), 0)
         w1_rows = w1.rearrange("(p j) n -> p j n", j=PACK)
+        nc.sync.dma_start(scales_all[:].bitcast(I32)[SCALE_ROW0:, :], x_scales[0].bitcast(I32))
         nc.sync.dma_start(offs_sb[:], offs)
-        nc.sync.dma_start(w1_raw[0][:], w1_rows[:, :, :W1_FRONT])
-        nc.sync.dma_start(pos_sb[0][:], pos1)
-        nc.sync.dma_start(pos_sb[1][:], pos2)
+        nc.sync.dma_start(words_all[:].bitcast(I32), x_words[0].bitcast(I32))
         nc.sync.dma_start(nxt_sb[0][:], nxt1)
         nc.sync.dma_start(nxt_sb[1][:], nxt2)
-        nc.sync.dma_start(scales_all[:].bitcast(I32)[0:P:8, :], x_scales[0].bitcast(I32))
-        nc.sync.dma_start(words_all[:].bitcast(I32), x_words[0].bitcast(I32))
-        nc.sync.dma_start(w1_raw[1][:], w1_rows[:, :, W1_FRONT:])
+        for i in range(2):
+            nc.sync.dma_start(w1_raw[i][:], w1_rows[:, :, w1_cuts[i] : w1_cuts[i + 1]])
+        nc.sync.dma_start(pos_sb[0][:], pos1)
+        nc.sync.dma_start(pos_sb[1][:], pos2)
         make_identity(nc, ident[:])
 
-        spread_exps = held([P, S], U8, "spread_exps")
-        nc.vector.tensor_copy(spread_exps[:], scales_all[:].indirect(offs_sb[:]))
+        picked_exps = held([P, S], U8, "picked_exps")
+        nc.vector.tensor_copy(picked_exps[:], scales_all[:].indirect(offs_sb[:]))
         for j in range(4):
-            nc.sync.dma_start(x_exps[:].bitcast(I32)[j:P:32, :], spread_exps[:].bitcast(I32)[8 * j : P : 32, :])
+            nc.sync.dma_start(x_exps[:].bitcast(I32)[j:P:32, :], picked_exps[:].bitcast(I32)[SCALE_ROW0 + j : P : 4, :])
 
-        stage = in_slot("late_terms", [P, 2 * LATE_PITCH + PACK * N], F32, "stage")
-        late = [stage[:, LATE_PITCH * d : LATE_PITCH * d + PACK * V_HALF] for d in range(2)]
-        gate_turned = [late[d][:, 3 * P : 3 * P + V_HALF] for d in range(2)]
-        w2_raw = stage[:, 2 * LATE_PITCH :].rearrange("p (t n) -> p t n", t=PACK)
+        stage = in_slot("late_terms", [P, 2 * PACK * V_HALF + PACK * N], F32, "stage")
+        both_late = stage[:, : 2 * PACK * V_HALF].rearrange("p (d c) -> p d c", d=2)
+        late = [both_late[:, d, :] for d in range(2)]
+        gate_turned = both_late[:, :, 3 * P : 3 * P + V_HALF]
+        w2_raw = stage[:, 2 * PACK * V_HALF :].rearrange("p (t n) -> p t n", t=PACK)
         gate_rows = gate.rearrange("d p v -> p d v")
-        w2_rows = w2.rearrange("(q u r e) n -> u q r (e n)", u=2, r=8, e=2)
-        for u in range(2):
-            nc.sync.dma_start(stage[:, 2 * LATE_PITCH + 2 * N * u :][:, : 2 * N], w2_rows[u])
-        both_late = stage[:, : 2 * LATE_PITCH].rearrange("p (d c) -> p d c", d=2)
-        nc.sync.dma_start(both_late[:, :, 3 * P : 3 * P + V_HALF], gate_rows[:, :, :V_HALF])
+        nc.sync.dma_start(gate_turned, gate_rows[:, :, :V_HALF])
+        w2_rows = w2.rearrange("(q t r) n -> t q r n", t=PACK, r=8)
+        for t in range(PACK):
+            nc.sync.dma_start(w2_raw[:, t, :], w2_rows[t])
 
-        front = W1_FRONT
-        staged = [held([P, front + PACK * P + PACK * N], BF16, "staged0"), held([P, front + PACK * P], BF16, "staged1")]
-        w1_grouped = [staged[t % 2][:, front * (1 - t // 2) :][:, : PACK * P] for t in range(PACK)]
+        staged = held([P, 2 * PACK * P], BF16, "staged")
+        w1_grouped = [staged[:, first : first + PACK * P] for first in (W1_FRONT, 0, PACK * P, 0)]
 
         def round_w1(copy, t, i):
-            raw = w1_raw[i][:].rearrange("p j (q u c n e) -> p u e q c j n", u=2, c=4, n=2, e=2)
-            dst = w1_grouped[t].rearrange("p (q c n j) -> p q c j n", c=4, n=2, j=PACK)
-            copy(dst[:, w1_cuts[i] // 32 : w1_cuts[i + 1] // 32], raw[:, t // 2, t % 2])
+            raw = w1_raw[i][:].rearrange("p j (q t c n) -> p t q c j n", t=PACK, c=2, n=4)
+            dst = w1_grouped[t].rearrange("p (q c n j) -> p q c j n", c=2, n=4, j=PACK)
+            copy(dst[:, w1_cuts[i] // 32 : w1_cuts[i + 1] // 32], raw[:, t])
 
-        for t in range(PACK):
-            round_w1(nc.scalar.copy, t, 0)
-        for t in range(2):
-            round_w1(nc.scalar.copy, t, 1)
+        for i in range(2):
+            round_w1(nc.scalar.copy, 0, i)
 
         x_codes = []
         for half in range(2):
             codes = held([P, HALF], U16, "x_codes%d" % half)
             nc.vector.tensor_copy(codes[:], words_all[:].indirect(entries(offs_sb, HALF * half, HALF)))
             x_codes.append(codes)
-        w1_q = [quantise(w1_grouped[t], P, "w1_%d" % t) for t in range(2)]
-        for t in range(2, PACK):
-            round_w1(nc.vector.tensor_copy, t, 1)
-        w1_q.extend(quantise(w1_grouped[t], P, "w1_%d" % t) for t in range(2, PACK))
+        w1_codes = [held([P, P], U32, "w1_codes%d" % t) for t in range(PACK - 1)]
+        w1_codes.append(in_slot("w2_grouped", [P, P], U32, "w1_codes3"))
+        w1_scales = [held([P, P], U8, "w1_scales%d" % t) for t in range(PACK)]
+        quantise(w1_grouped[0], w1_codes[0][:], w1_scales[0][:])
+        for tiles in ((1, 2), (3,)):
+            for t in tiles:
+                for i in range(2):
+                    round_w1(nc.vector.tensor_copy, t, i)
+            for t in tiles:
+                quantise(w1_grouped[t], w1_codes[t][:], w1_scales[t][:])
 
         late_gates = in_slot("late_gates", [P, 2 * V_HALF + 2 * U], F32, "late_gates")
         gate_direct = late_gates[:, : 2 * V_HALF].rearrange("p (d v) -> p d v", d=2)
@@ -132,7 +128,6 @@ def tile_picked_hop2_gelu_p_kernel(
         h = []
         for t in range(PACK):
             h_t = held([P, S], F32, "h%d" % t)
-            codes, scales = w1_q[t]
             if t == 0:
                 pieces = [(0, HALF // 2), (HALF // 2, HALF // 2), (HALF, HALF)]
             else:
@@ -142,8 +137,8 @@ def tile_picked_hop2_gelu_p_kernel(
                 cols = slice(c0 % HALF, c0 % HALF + width)
                 nc.tensor.matmul_mx(
                     out=acc[:],
-                    lhsT=codes[:].bitcast(FP8X4),
-                    lhsT_scale=scales[:],
+                    lhsT=w1_codes[t][:].bitcast(FP8X4),
+                    lhsT_scale=w1_scales[t][:],
                     rhs=x_codes[c0 // HALF][:, cols].bitcast(FP4X4),
                     rhs_scale=x_exps[:, c0 : c0 + width],
                     start=True,
@@ -152,39 +147,44 @@ def tile_picked_hop2_gelu_p_kernel(
                 nc.scalar.activation(h_t[:, c0 : c0 + width], acc[:], ACT.Gelu_apprx_tanh)
             h.append(h_t)
 
-        w2_grouped = staged[0][:, PACK * P : PACK * (P + N)]
-        nc.vector.tensor_copy(
-            w2_grouped.rearrange("p (c n t) -> p c t n", n=4, t=PACK), w2_raw.rearrange("p t (c n) -> p c t n", n=4)
+        w2_grouped = in_slot("w2_grouped", [P, PACK * N], BF16, "w2_grouped")
+        nc.scalar.copy(
+            w2_grouped[:].rearrange("p (c n t) -> p c t n", n=4, t=PACK),
+            w2_raw.rearrange("p t (c n) -> p c t n", n=4),
         )
-        w2_codes, w2_scales = quantise(w2_grouped, N, "w2")
+        w2_codes = held([P, N], U32, "w2_codes")
+        w2_scales = held([P, N], U8, "w2_scales")
+        quantise(w2_grouped[:], w2_codes[:], w2_scales[:])
 
         def weighted_gather(dst, t, d, v0, width, weights):
             nc.vector.tensor_tensor(dst, h[t][:].indirect(entries(pos_sb[d], v0, width)), weights, MULT)
 
         g = [held([P, V], F32, "g%d" % m) for m in range(2)]
+        z_codes = held([P, V], U32, "z_codes")
+        z_scales = held([P, V], U8, "z_scales")
 
-        def second_layer(codes, scales, v0, width):
-            for m in range(2):
-                acc = bank([P, width])
-                nc.tensor.matmul_mx(
-                    out=acc[:],
-                    lhsT=w2_codes[:, P * m : P * (m + 1)].bitcast(FP8X4),
-                    lhsT_scale=w2_scales[:, P * m : P * (m + 1)],
-                    rhs=codes[:].bitcast(FP8X4),
-                    rhs_scale=scales[:],
-                    start=True,
-                    stop=True,
-                )
-                nc.scalar.activation(g[m][:, v0 : v0 + width], acc[:], ACT.Relu)
+        def second_layer(m, v0, width, acc):
+            cols = slice(v0, v0 + width)
+            nc.tensor.matmul_mx(
+                out=acc,
+                lhsT=w2_codes[:, P * m : P * (m + 1)].bitcast(FP8X4),
+                lhsT_scale=w2_scales[:, P * m : P * (m + 1)],
+                rhs=z_codes[:, cols].bitcast(FP8X4),
+                rhs_scale=z_scales[:, cols],
+                start=True,
+                stop=True,
+            )
+            nc.scalar.activation(g[m][:, cols], acc, ACT.Relu)
 
         z_sum = [psum.tile([P, H], F32, name="z_sum%d" % b) for b in range(2)]
         z_rows = [held([P, 2, P, 2], BF16, "z_rows%d" % b) for b in range(2)]
         for t in range(PACK):
-            parts = []
+            if t == 2:
+                parts = [late[d][:, :V_HALF] for d in range(2)]
+            else:
+                parts = [held([P, V_HALF], F32, "part%d_%d" % (t, d))[:] for d in range(2)]
             for d in range(2):
-                part = held([P, V_HALF], F32, "part%d_%d" % (t, d))
-                weighted_gather(part[:], t, d, 0, V_HALF, gate_turned[d])
-                parts.append(part)
+                weighted_gather(parts[d], t, d, 0, V_HALF, gate_turned[:, d, :])
             for b in range(2):
                 for d in range(2):
                     nc.tensor.matmul(
@@ -195,49 +195,46 @@ def tile_picked_hop2_gelu_p_kernel(
                         stop=(d == 1),
                         is_transpose=True,
                     )
-            if t % 2 == 1:
-                u = t // 2
-                for b in range(2):
+                if t % 2 == 1:
+                    u = t // 2
                     nc.scalar.copy(
                         z_rows[b][:, u, :, :],
                         z_sum[b][:, 2 * P * u : 2 * P * (u + 1)].rearrange("v (e p) -> v p e", e=2),
                     )
 
-        early_codes = held([P, V_HALF], U32, "early_codes")
-        early_scales = held([P, V_HALF], U8, "early_scales")
         for b in range(2):
-            first = LATE_PITCH * b + PACK * V_HALF - OVERLAP[b]
-            words = stage[:, first : first + 2 * P]
+            words = late[b][:, (PACK - 1) * V_HALF :]
             turned = bank([P, 2, P])
             pairs = z_rows[b][:].rearrange("v u p e -> v (u p e)").bitcast(F32)
             for u in range(2):
                 nc.tensor.transpose(turned[:, u, :], pairs[:, P * u : P * (u + 1)], ident[:])
             nc.scalar.copy(words.rearrange("p (v u) -> p v u", u=2), turned[:].rearrange("p u v -> p v u"))
             cols = slice(P * b, P * (b + 1))
-            nc.vector.quantize_mx(
-                out=early_codes[:, cols].bitcast(FP8X4), scales=early_scales[:, cols], in_=words.bitcast(BF16)
-            )
-        second_layer(early_codes, early_scales, 0, V_HALF)
+            quantise(words.bitcast(BF16), z_codes[:, cols], z_scales[:, cols])
+        for m in range(2):
+            second_layer(m, 0, V_HALF, bank([P, V_HALF])[:])
 
         for t in range(PACK - 1):
             for d in range(2):
                 weighted_gather(late[d][:, t * V_HALF : (t + 1) * V_HALF], t, d, V_HALF, V_HALF, gate_direct[:, d, :])
-        v0 = 0
-        for width in LATE_GROUPS:
-            cols = slice(v0, v0 + width)
-            terms = [late[d].rearrange("p (t v) -> p t v", t=PACK)[:, :, cols] for d in range(2)]
+        terms = [late[d].rearrange("p (t b c v) -> p b c t v", t=PACK, b=2, v=4) for d in range(2)]
+        for b in range(2):
             for d in range(2):
-                weighted_gather(terms[d][:, PACK - 1, :], PACK - 1, d, V_HALF + v0, width, gate_direct[:, d, cols])
-            grouped = held([P, PACK * width], BF16, "late_grouped%d" % v0)
+                c0 = (PACK - 1) * V_HALF + b * P
+                weighted_gather(
+                    late[d][:, c0 : c0 + P], PACK - 1, d, V_HALF + b * P, P, gate_direct[:, d, b * P : (b + 1) * P]
+                )
+        late_grouped = [held([P, PACK * P], BF16, "late_grouped%d" % b) for b in range(2)]
+        for b in range(2):
             nc.vector.tensor_tensor(
-                grouped[:].rearrange("p (c v t) -> p c t v", v=4, t=PACK),
-                terms[0].rearrange("p t (c v) -> p c t v", v=4),
-                terms[1].rearrange("p t (c v) -> p c t v", v=4),
-                ADD,
+                late_grouped[b][:].rearrange("p (c v t) -> p c t v", v=4, t=PACK), terms[0][:, b], terms[1][:, b], ADD
             )
-            codes, scales = quantise(grouped[:], width, "z%d" % v0)
-            second_layer(codes, scales, V_HALF + v0, width)
-            v0 = v0 + width
+        for b in range(2):
+            cols = slice(V_HALF + P * b, V_HALF + P * (b + 1))
+            quantise(late_grouped[b][:], z_codes[:, cols], z_scales[:, cols])
+        for b in range(2):
+            second_layer(0, V_HALF + P * b, P, bank([P, P])[:])
+        second_layer(1, V_HALF, V_HALF, bank([P, V_HALF])[:])
 
         roots = []
         for m in range(2):

@@ -74,6 +74,9 @@ def tile_picked_hop2_gelu_p_kernel(
             nc.sync.dma_start(w1_raw[i][:], w1_rows[:, :, w1_cuts[i] : w1_cuts[i + 1]])
         nc.sync.dma_start(pos_sb[0][:], pos1)
         nc.sync.dma_start(pos_sb[1][:], pos2)
+        warm = held([P, 2], F32, "warm")
+        nc.gpsimd.memset(warm[:, 0:1], 0.0)
+        nc.scalar.activation(warm[:, 1:2], warm[:, 0:1], ACT.Gelu_apprx_tanh)
         make_identity(nc, ident[:])
 
         picked_exps = held([P, S], U8, "picked_exps")

@@ -22,10 +22,12 @@ P = 128
 PACK = 4
 LIST_ROWS = 16
 HALF = S // 2
-V_HALF = V // 2
+GROUPS = 3
+V_TURNED = GROUPS * P
+LATE = PACK * P
 SCALE_ROW0 = P - 16
 W1_FRONT = 384
-RING_BANKS = 6
+RING_BANKS = 8 - GROUPS
 
 
 def tile_picked_hop2_gelu_p_kernel(
@@ -84,19 +86,19 @@ def tile_picked_hop2_gelu_p_kernel(
         for j in range(4):
             nc.sync.dma_start(x_exps[:].bitcast(I32)[j:P:32, :], picked_exps[:].bitcast(I32)[SCALE_ROW0 + j : P : 4, :])
 
-        stage = in_slot("late_terms", [P, 2 * PACK * V_HALF + PACK * N], F32, "stage")
-        both_late = stage[:, : 2 * PACK * V_HALF].rearrange("p (d c) -> p d c", d=2)
+        stage = in_slot("late_terms", [P, 2 * LATE + PACK * N], F32, "stage")
+        both_late = stage[:, : 2 * LATE].rearrange("p (d c) -> p d c", d=2)
         late = [both_late[:, d, :] for d in range(2)]
-        gate_turned = both_late[:, :, 3 * P : 3 * P + V_HALF]
-        w2_raw = stage[:, 2 * PACK * V_HALF :].rearrange("p (t n) -> p t n", t=PACK)
+        gate_turned = both_late[:, :, :V_TURNED]
+        w2_raw = stage[:, 2 * LATE :].rearrange("p (t n) -> p t n", t=PACK)
         gate_rows = gate.rearrange("d p v -> p d v")
-        nc.sync.dma_start(gate_turned, gate_rows[:, :, :V_HALF])
+        nc.sync.dma_start(gate_turned, gate_rows[:, :, :V_TURNED])
         w2_rows = w2.rearrange("(q t r) n -> t q r n", t=PACK, r=8)
         for t in range(PACK):
             nc.sync.dma_start(w2_raw[:, t, :], w2_rows[t])
 
         staged = held([P, 2 * PACK * P], BF16, "staged")
-        w1_grouped = [staged[:, first : first + PACK * P] for first in (W1_FRONT, 0, PACK * P, 0)]
+        w1_grouped = [staged[:, first : first + PACK * P] for first in (PACK * P // 2, 0, PACK * P, 0)]
 
         def round_w1(copy, t, i):
             raw = w1_raw[i][:].rearrange("p j (q t c n) -> p t q c j n", t=PACK, c=2, n=4)
@@ -115,24 +117,26 @@ def tile_picked_hop2_gelu_p_kernel(
         w1_codes.append(in_slot("w2_grouped", [P, P], U32, "w1_codes3"))
         w1_scales = [held([P, P], U8, "w1_scales%d" % t) for t in range(PACK)]
         quantise(w1_grouped[0], w1_codes[0][:], w1_scales[0][:])
-        for tiles in ((1, 2), (3,)):
-            for t in tiles:
-                for i in range(2):
-                    round_w1(nc.vector.tensor_copy, t, i)
-            for t in tiles:
-                quantise(w1_grouped[t], w1_codes[t][:], w1_scales[t][:])
+        for i in range(2):
+            round_w1(nc.scalar.copy, 2, i)
+        for t in (1, 3):
+            for i in range(2):
+                round_w1(nc.vector.tensor_copy, t, i)
+            if t == 3:
+                quantise(w1_grouped[2], w1_codes[2][:], w1_scales[2][:])
+            quantise(w1_grouped[t], w1_codes[t][:], w1_scales[t][:])
 
-        late_gates = in_slot("late_gates", [P, 2 * V_HALF + 2 * U], F32, "late_gates")
-        gate_direct = late_gates[:, : 2 * V_HALF].rearrange("p (d v) -> p d v", d=2)
-        gate2_sb = late_gates[:, 2 * V_HALF :].rearrange("p (d r) -> p d r", d=2)
-        nc.sync.dma_start(gate_direct, gate_rows[:, :, V_HALF:])
+        late_gates = in_slot("late_gates", [P, 2 * P + 2 * U], F32, "late_gates")
+        gate_direct = late_gates[:, : 2 * P].rearrange("p (d v) -> p d v", d=2)
+        gate2_sb = late_gates[:, 2 * P :].rearrange("p (d r) -> p d r", d=2)
+        nc.sync.dma_start(gate_direct, gate_rows[:, :, V_TURNED:])
         nc.sync.dma_start(gate2_sb, gate2.rearrange("d p r -> p d r"))
 
         h = []
         for t in range(PACK):
             h_t = held([P, S], F32, "h%d" % t)
             if t == 0:
-                pieces = [(0, HALF // 2), (HALF // 2, HALF // 2), (HALF, HALF)]
+                pieces = [(0, P), (P, P), (2 * P, 2 * P), (4 * P, 2 * P), (6 * P, 2 * P)]
             else:
                 pieces = [(0, HALF), (HALF, HALF)]
             for c0, width in pieces:
@@ -179,20 +183,23 @@ def tile_picked_hop2_gelu_p_kernel(
             )
             nc.scalar.activation(g[m][:, cols], acc, ACT.Relu)
 
-        z_sum = [psum.tile([P, H], F32, name="z_sum%d" % b) for b in range(2)]
-        z_rows = [held([P, 2, P, 2], BF16, "z_rows%d" % b) for b in range(2)]
+        z_sum = [psum.tile([P, H], F32, name="z_sum%d" % b) for b in range(GROUPS)]
+        z_pairs = [[held([P, P], F32, "z_pairs%d%d" % (b, u))[:] for u in range(2)] for b in (0, 2)]
+        z_pairs.insert(1, [late[u][:, V_TURNED:] for u in range(2)])
         for t in range(PACK):
-            if t == 2:
-                parts = [late[d][:, :V_HALF] for d in range(2)]
-            else:
-                parts = [held([P, V_HALF], F32, "part%d_%d" % (t, d))[:] for d in range(2)]
-            for d in range(2):
-                weighted_gather(parts[d], t, d, 0, V_HALF, gate_turned[:, d, :])
-            for b in range(2):
+            parts = [held([P, V_TURNED], F32, "part%d_%d" % (t, d))[:] for d in range(2)]
+            if t < PACK - 1:
+                for d in range(2):
+                    weighted_gather(parts[d], t, d, 0, V_TURNED, gate_turned[:, d, :])
+            for b in range(GROUPS):
+                cols = slice(P * b, P * (b + 1))
+                if t == PACK - 1:
+                    for d in range(2):
+                        weighted_gather(parts[d][:, cols], t, d, P * b, P, gate_turned[:, d, cols])
                 for d in range(2):
                     nc.tensor.matmul(
                         z_sum[b][:, P * t : P * (t + 1)],
-                        parts[d][:, P * b : P * (b + 1)],
+                        parts[d][:, cols],
                         ident[:],
                         start=(d == 0),
                         stop=(d == 1),
@@ -201,43 +208,50 @@ def tile_picked_hop2_gelu_p_kernel(
                 if t % 2 == 1:
                     u = t // 2
                     nc.scalar.copy(
-                        z_rows[b][:, u, :, :],
+                        z_pairs[b][u].bitcast(BF16).rearrange("v (p e) -> v p e", e=2),
                         z_sum[b][:, 2 * P * u : 2 * P * (u + 1)].rearrange("v (e p) -> v p e", e=2),
                     )
 
-        for b in range(2):
-            words = late[b][:, (PACK - 1) * V_HALF :]
+        words = [held([P, 2 * P], F32, "words%d" % b)[:] for b in range(GROUPS)]
+        for b in range(GROUPS):
             turned = bank([P, 2, P])
-            pairs = z_rows[b][:].rearrange("v u p e -> v (u p e)").bitcast(F32)
             for u in range(2):
-                nc.tensor.transpose(turned[:, u, :], pairs[:, P * u : P * (u + 1)], ident[:])
-            nc.scalar.copy(words.rearrange("p (v u) -> p v u", u=2), turned[:].rearrange("p u v -> p v u"))
+                nc.tensor.transpose(turned[:, u, :], z_pairs[b][u], ident[:])
+            nc.scalar.copy(words[b].rearrange("p (v u) -> p v u", u=2), turned[:].rearrange("p u v -> p v u"))
+
+        def quantise_group(b, grouped):
             cols = slice(P * b, P * (b + 1))
-            quantise(words.bitcast(BF16), z_codes[:, cols], z_scales[:, cols])
-        for m in range(2):
-            second_layer(m, 0, V_HALF, bank([P, V_HALF])[:])
+            quantise(grouped, z_codes[:, cols], z_scales[:, cols])
 
         for t in range(PACK - 1):
             for d in range(2):
-                weighted_gather(late[d][:, t * V_HALF : (t + 1) * V_HALF], t, d, V_HALF, V_HALF, gate_direct[:, d, :])
-        terms = [late[d].rearrange("p (t b c v) -> p b c t v", t=PACK, b=2, v=4) for d in range(2)]
+                weighted_gather(late[d][:, t * P : (t + 1) * P], t, d, V_TURNED, P, gate_direct[:, d, :])
         for b in range(2):
+            quantise_group(b, words[b].bitcast(BF16))
+        for m in range(2):
+            second_layer(m, 0, 2 * P, bank([P, 2 * P])[:])
+        half = P // 2
+        for a in range(2):
             for d in range(2):
-                c0 = (PACK - 1) * V_HALF + b * P
+                c0 = (PACK - 1) * P + half * a
                 weighted_gather(
-                    late[d][:, c0 : c0 + P], PACK - 1, d, V_HALF + b * P, P, gate_direct[:, d, b * P : (b + 1) * P]
+                    late[d][:, c0 : c0 + half],
+                    PACK - 1,
+                    d,
+                    V_TURNED + half * a,
+                    half,
+                    gate_direct[:, d, half * a : half * (a + 1)],
                 )
-        late_grouped = [held([P, PACK * P], BF16, "late_grouped%d" % b) for b in range(2)]
-        for b in range(2):
-            nc.vector.tensor_tensor(
-                late_grouped[b][:].rearrange("p (c v t) -> p c t v", v=4, t=PACK), terms[0][:, b], terms[1][:, b], ADD
-            )
-        for b in range(2):
-            cols = slice(V_HALF + P * b, V_HALF + P * (b + 1))
-            quantise(late_grouped[b][:], z_codes[:, cols], z_scales[:, cols])
-        for b in range(2):
-            second_layer(0, V_HALF + P * b, P, bank([P, P])[:])
-        second_layer(1, V_HALF, V_HALF, bank([P, V_HALF])[:])
+        terms = [late[d].rearrange("p (t a c v) -> p a c t v", t=PACK, a=2, v=4) for d in range(2)]
+        late_grouped = held([P, PACK * P], BF16, "late_grouped")
+        for a in range(2):
+            dst = late_grouped[:].rearrange("p (a c v t) -> p a c t v", a=2, v=4, t=PACK)
+            nc.vector.tensor_tensor(dst[:, a], terms[0][:, a], terms[1][:, a], ADD)
+        quantise_group(2, words[2].bitcast(BF16))
+        quantise_group(3, late_grouped[:])
+        for b in (2, 3):
+            second_layer(0, P * b, P, bank([P, P])[:])
+        second_layer(1, 2 * P, 2 * P, bank([P, 2 * P])[:])
 
         roots = []
         for m in range(2):

@@ -26,7 +26,8 @@ GROUPS = 3
 V_TURNED = GROUPS * P
 LATE = PACK * P
 SCALE_ROW0 = P - 16
-W1_FRONT = 384
+W1_SHORT = 128
+RUN = 8
 RING_BANKS = 8 - GROUPS
 
 
@@ -60,8 +61,12 @@ def tile_picked_hop2_gelu_p_kernel(
         words_all = in_slot("late_gates", [P, T], U16, "words_all")
         scales_all = in_slot("late_terms", [P, T], U8, "scales_all")
         x_exps = held([P, S], U8, "x_exps")
-        w1_cuts = [0, W1_FRONT, H]
-        w1_raw = [held([P, PACK, w1_cuts[i + 1] - w1_cuts[i]], F32, "w1_raw%d" % i) for i in range(2)]
+        w1_cols = [slice(W1_SHORT, H), slice(0, W1_SHORT)]
+        short_room = held([P, 2 * P - RUN + PACK * W1_SHORT], F32, "short_room")
+        w1_raw = [
+            held([P, PACK, H - W1_SHORT], F32, "w1_long")[:],
+            short_room[:, 2 * P - RUN :].rearrange("p (j n) -> p j n", j=PACK),
+        ]
         ident = held([P, P], F32, "ident")
 
         nc.vector.memset(scales_all[:].bitcast(I32)[:SCALE_ROW0, :], 0)
@@ -73,7 +78,7 @@ def tile_picked_hop2_gelu_p_kernel(
         nc.sync.dma_start(nxt_sb[0][:], nxt1)
         nc.sync.dma_start(nxt_sb[1][:], nxt2)
         for i in range(2):
-            nc.sync.dma_start(w1_raw[i][:], w1_rows[:, :, w1_cuts[i] : w1_cuts[i + 1]])
+            nc.sync.dma_start(w1_raw[i], w1_rows[:, :, w1_cols[i]])
         nc.sync.dma_start(pos_sb[0][:], pos1)
         nc.sync.dma_start(pos_sb[1][:], pos2)
         warm = held([P, 2], F32, "warm")
@@ -97,13 +102,18 @@ def tile_picked_hop2_gelu_p_kernel(
         for t in range(PACK):
             nc.sync.dma_start(w2_raw[:, t, :], w2_rows[t])
 
-        staged = held([P, 2 * PACK * P], BF16, "staged")
-        w1_grouped = [staged[:, first : first + PACK * P] for first in (PACK * P // 2, 0, PACK * P, 0)]
+        staged = held([P, 9 * P], BF16, "staged")
+        w1_grouped = [
+            staged[:, 3 * P : 7 * P],
+            staged[:, : 4 * P],
+            short_room[:, : 2 * P].bitcast(BF16),
+            staged[:, 5 * P :],
+        ]
 
         def round_w1(copy, t, i):
-            raw = w1_raw[i][:].rearrange("p j (q t c n) -> p t q c j n", t=PACK, c=2, n=4)
+            raw = w1_raw[i].rearrange("p j (q t c n) -> p t q c j n", t=PACK, c=2, n=4)
             dst = w1_grouped[t].rearrange("p (q c n j) -> p q c j n", c=2, n=4, j=PACK)
-            copy(dst[:, w1_cuts[i] // 32 : w1_cuts[i + 1] // 32], raw[:, t])
+            copy(dst[:, w1_cols[i].start // 32 : w1_cols[i].stop // 32], raw[:, t])
 
         for i in range(2):
             round_w1(nc.scalar.copy, 0, i)
@@ -122,8 +132,7 @@ def tile_picked_hop2_gelu_p_kernel(
         for t in (1, 3):
             for i in range(2):
                 round_w1(nc.vector.tensor_copy, t, i)
-            if t == 3:
-                quantise(w1_grouped[2], w1_codes[2][:], w1_scales[2][:])
+        for t in range(1, PACK):
             quantise(w1_grouped[t], w1_codes[t][:], w1_scales[t][:])
 
         late_gates = in_slot("late_gates", [P, 2 * P + 2 * U], F32, "late_gates")
@@ -154,14 +163,15 @@ def tile_picked_hop2_gelu_p_kernel(
                 nc.scalar.activation(h_t[:, c0 : c0 + width], acc[:], ACT.Gelu_apprx_tanh)
             h.append(h_t)
 
-        w2_grouped = in_slot("w2_grouped", [P, PACK * N], BF16, "w2_grouped")
-        nc.scalar.copy(
-            w2_grouped[:].rearrange("p (c n t) -> p c t n", n=4, t=PACK),
-            w2_raw.rearrange("p t (c n) -> p c t n", n=4),
-        )
-        w2_codes = held([P, N], U32, "w2_codes")
-        w2_scales = held([P, N], U8, "w2_scales")
-        quantise(w2_grouped[:], w2_codes[:], w2_scales[:])
+        w2_grouped = in_slot("w2_grouped", [P, 2, PACK * P], BF16, "w2_grouped")
+        w2_codes = [held([P, P], U32, "w2_codes0")]
+        w2_scales = [held([P, P], U8, "w2_scales%d" % m) for m in range(2)]
+
+        def round_w2(m):
+            nc.scalar.copy(
+                w2_grouped[:, m, :].rearrange("p (c n t) -> p c t n", n=4, t=PACK),
+                w2_raw[:, :, P * m : P * (m + 1)].rearrange("p t (c n) -> p c t n", n=4),
+            )
 
         def weighted_gather(dst, t, d, v0, width, weights):
             nc.vector.tensor_tensor(dst, h[t][:].indirect(entries(pos_sb[d], v0, width)), weights, MULT)
@@ -174,8 +184,8 @@ def tile_picked_hop2_gelu_p_kernel(
             cols = slice(v0, v0 + width)
             nc.tensor.matmul_mx(
                 out=acc,
-                lhsT=w2_codes[:, P * m : P * (m + 1)].bitcast(FP8X4),
-                lhsT_scale=w2_scales[:, P * m : P * (m + 1)],
+                lhsT=w2_codes[m][:].bitcast(FP8X4),
+                lhsT_scale=w2_scales[m][:],
                 rhs=z_codes[:, cols].bitcast(FP8X4),
                 rhs_scale=z_scales[:, cols],
                 start=True,
@@ -211,8 +221,12 @@ def tile_picked_hop2_gelu_p_kernel(
                         z_pairs[b][u].bitcast(BF16).rearrange("v (p e) -> v p e", e=2),
                         z_sum[b][:, 2 * P * u : 2 * P * (u + 1)].rearrange("v (e p) -> v p e", e=2),
                     )
+            if t == 1:
+                round_w2(0)
+                quantise(w2_grouped[:, 0, :], w2_codes[0][:], w2_scales[0][:])
+                round_w2(1)
 
-        words = [held([P, 2 * P], F32, "words%d" % b)[:] for b in range(GROUPS)]
+        words = [in_slot("words%d" % b, [P, 2 * P], F32, "words%d" % b)[:] for b in range(GROUPS)]
         for b in range(GROUPS):
             turned = bank([P, 2, P])
             for u in range(2):
@@ -228,8 +242,7 @@ def tile_picked_hop2_gelu_p_kernel(
                 weighted_gather(late[d][:, t * P : (t + 1) * P], t, d, V_TURNED, P, gate_direct[:, d, :])
         for b in range(2):
             quantise_group(b, words[b].bitcast(BF16))
-        for m in range(2):
-            second_layer(m, 0, 2 * P, bank([P, 2 * P])[:])
+        second_layer(0, 0, 2 * P, bank([P, 2 * P])[:])
         half = P // 2
         for a in range(2):
             for d in range(2):
@@ -251,7 +264,10 @@ def tile_picked_hop2_gelu_p_kernel(
         quantise_group(3, late_grouped[:])
         for b in (2, 3):
             second_layer(0, P * b, P, bank([P, P])[:])
-        second_layer(1, 2 * P, 2 * P, bank([P, 2 * P])[:])
+        w2_codes.append(in_slot("words2", [P, P], U32, "w2_codes1"))
+        quantise(w2_grouped[:, 1, :], w2_codes[1][:], w2_scales[1][:])
+        for b in (0, 2):
+            second_layer(1, P * b, 2 * P, bank([P, 2 * P])[:])
 
         roots = []
         for m in range(2):
@@ -259,7 +275,8 @@ def tile_picked_hop2_gelu_p_kernel(
                 root = held([P, U], F32, "root%d%d" % (m, d))
                 nc.vector.tensor_tensor(root[:], g[m][:].indirect(nxt_sb[d][:]), gate2_sb[:, d, :], MULT)
                 roots.append(root)
-        for m in range(2):
-            result = held([P, U], F32, "result%d" % m)
-            nc.vector.tensor_tensor(result[:], roots[2 * m][:], roots[2 * m + 1][:], ADD)
-            nc.sync.dma_start(out[P * m : P * (m + 1), :], result[:])
+        for m, r0, width in ((0, 0, U), (1, 0, U // 2), (1, U // 2, U // 2)):
+            cols = slice(r0, r0 + width)
+            result = held([P, width], F32, "result%d_%d" % (m, r0))
+            nc.vector.tensor_tensor(result[:], roots[2 * m][:, cols], roots[2 * m + 1][:, cols], ADD)
+            nc.sync.dma_start(out[P * m : P * (m + 1), cols], result[:])

@@ -22,8 +22,9 @@ P = 128
 PACK = 4
 LIST_ROWS = 16
 HALF = S // 2
-GROUPS = 3
-V_TURNED = GROUPS * P
+V_DIRECT = P // 2
+V_TURNED = V - V_DIRECT
+GROUPS = 4
 LATE = PACK * P
 SCALE_ROW0 = P - 16
 W1_SHORT = 128
@@ -135,9 +136,9 @@ def tile_picked_hop2_gelu_p_kernel(
         for t in range(1, PACK):
             quantise(w1_grouped[t], w1_codes[t][:], w1_scales[t][:])
 
-        late_gates = in_slot("late_gates", [P, 2 * P + 2 * U], F32, "late_gates")
-        gate_direct = late_gates[:, : 2 * P].rearrange("p (d v) -> p d v", d=2)
-        gate2_sb = late_gates[:, 2 * P :].rearrange("p (d r) -> p d r", d=2)
+        late_gates = in_slot("late_gates", [P, 2 * V_DIRECT + 2 * U], F32, "late_gates")
+        gate_direct = late_gates[:, : 2 * V_DIRECT].rearrange("p (d v) -> p d v", d=2)
+        gate2_sb = late_gates[:, 2 * V_DIRECT :].rearrange("p (d r) -> p d r", d=2)
         nc.sync.dma_start(gate_direct, gate_rows[:, :, V_TURNED:])
         nc.sync.dma_start(gate2_sb, gate2.rearrange("d p r -> p d r"))
 
@@ -193,23 +194,27 @@ def tile_picked_hop2_gelu_p_kernel(
             )
             nc.scalar.activation(g[m][:, cols], acc, ACT.Relu)
 
+        starts = [2 * P, V_TURNED - P, 0, P]
+        last_runs = {0: slice(2 * P, V_TURNED), 2: slice(0, P), 3: slice(P, 2 * P)}
         z_sum = [psum.tile([P, H], F32, name="z_sum%d" % b) for b in range(GROUPS)]
-        z_pairs = [[held([P, P], F32, "z_pairs%d%d" % (b, u))[:] for u in range(2)] for b in (0, 2)]
-        z_pairs.insert(1, [late[u][:, V_TURNED:] for u in range(2)])
+        z_pairs = [
+            [in_slot("pairs%d%d" % (b, u), [P, P], F32, "z_pairs%d%d" % (b, u))[:] for u in range(2)]
+            for b in range(GROUPS)
+        ]
         for t in range(PACK):
             parts = [held([P, V_TURNED], F32, "part%d_%d" % (t, d))[:] for d in range(2)]
             if t < PACK - 1:
                 for d in range(2):
                     weighted_gather(parts[d], t, d, 0, V_TURNED, gate_turned[:, d, :])
             for b in range(GROUPS):
-                cols = slice(P * b, P * (b + 1))
-                if t == PACK - 1:
+                if t == PACK - 1 and b in last_runs:
+                    run = last_runs[b]
                     for d in range(2):
-                        weighted_gather(parts[d][:, cols], t, d, P * b, P, gate_turned[:, d, cols])
+                        weighted_gather(parts[d][:, run], t, d, run.start, run.stop - run.start, gate_turned[:, d, run])
                 for d in range(2):
                     nc.tensor.matmul(
                         z_sum[b][:, P * t : P * (t + 1)],
-                        parts[d][:, cols],
+                        parts[d][:, starts[b] : starts[b] + P],
                         ident[:],
                         start=(d == 0),
                         stop=(d == 1),
@@ -226,48 +231,44 @@ def tile_picked_hop2_gelu_p_kernel(
                 quantise(w2_grouped[:, 0, :], w2_codes[0][:], w2_scales[0][:])
                 round_w2(1)
 
-        words = [in_slot("words%d" % b, [P, 2 * P], F32, "words%d" % b)[:] for b in range(GROUPS)]
+        fresh = [P, P // 2, P, P]
+        words = [in_slot("words%d" % b, [P, 2 * fresh[b]], F32, "words%d" % b)[:] for b in range(GROUPS)]
         for b in range(GROUPS):
             turned = bank([P, 2, P])
             for u in range(2):
                 nc.tensor.transpose(turned[:, u, :], z_pairs[b][u], ident[:])
-            nc.scalar.copy(words[b].rearrange("p (v u) -> p v u", u=2), turned[:].rearrange("p u v -> p v u"))
+            nc.scalar.copy(
+                words[b].rearrange("p (v u) -> p v u", u=2), turned[:, :, P - fresh[b] :].rearrange("p u v -> p v u")
+            )
 
-        def quantise_group(b, grouped):
-            cols = slice(P * b, P * (b + 1))
+        def quantise_z(v0, width, grouped):
+            cols = slice(v0, v0 + width)
             quantise(grouped, z_codes[:, cols], z_scales[:, cols])
 
-        for t in range(PACK - 1):
+        def quantise_group(b):
+            quantise_z(starts[b] + P - fresh[b], fresh[b], words[b].bitcast(BF16))
+
+        for t in range(PACK):
             for d in range(2):
-                weighted_gather(late[d][:, t * P : (t + 1) * P], t, d, V_TURNED, P, gate_direct[:, d, :])
+                dst = late[d][:, t * V_DIRECT : (t + 1) * V_DIRECT]
+                weighted_gather(dst, t, d, V_TURNED, V_DIRECT, gate_direct[:, d, :])
         for b in range(2):
-            quantise_group(b, words[b].bitcast(BF16))
-        second_layer(0, 0, 2 * P, bank([P, 2 * P])[:])
-        half = P // 2
-        for a in range(2):
-            for d in range(2):
-                c0 = (PACK - 1) * P + half * a
-                weighted_gather(
-                    late[d][:, c0 : c0 + half],
-                    PACK - 1,
-                    d,
-                    V_TURNED + half * a,
-                    half,
-                    gate_direct[:, d, half * a : half * (a + 1)],
-                )
-        terms = [late[d].rearrange("p (t a c v) -> p a c t v", t=PACK, a=2, v=4) for d in range(2)]
-        late_grouped = held([P, PACK * P], BF16, "late_grouped")
-        for a in range(2):
-            dst = late_grouped[:].rearrange("p (a c v t) -> p a c t v", a=2, v=4, t=PACK)
-            nc.vector.tensor_tensor(dst[:, a], terms[0][:, a], terms[1][:, a], ADD)
-        quantise_group(2, words[2].bitcast(BF16))
-        quantise_group(3, late_grouped[:])
-        for b in (2, 3):
-            second_layer(0, P * b, P, bank([P, P])[:])
-        w2_codes.append(in_slot("words2", [P, P], U32, "w2_codes1"))
+            quantise_group(b)
+        second_layer(0, 2 * P, P, bank([P, P])[:])
+        terms = [late[d][:, : PACK * V_DIRECT].rearrange("p (t c v) -> p c t v", t=PACK, v=4) for d in range(2)]
+        late_grouped = in_slot("pairs21", [P, PACK * V_DIRECT], BF16, "late_grouped")
+        nc.vector.tensor_tensor(
+            late_grouped[:].rearrange("p (c v t) -> p c t v", v=4, t=PACK), terms[0], terms[1], ADD
+        )
+        quantise_group(2)
+        quantise_z(V_TURNED, V_DIRECT, late_grouped[:])
+        quantise_group(3)
+        for v0 in (0, 3 * P, P):
+            second_layer(0, v0, P, bank([P, P])[:])
+        w2_codes.append(in_slot("words3", [P, P], U32, "w2_codes1"))
         quantise(w2_grouped[:, 1, :], w2_codes[1][:], w2_scales[1][:])
-        for b in (0, 2):
-            second_layer(1, P * b, 2 * P, bank([P, 2 * P])[:])
+        for v0 in (2 * P, 0):
+            second_layer(1, v0, 2 * P, bank([P, 2 * P])[:])
 
         roots = []
         for m in range(2):

@@ -20,16 +20,16 @@ ADD = mybir.AluOpType.add
 
 P = 128
 PACK = 4
+BLOCK = 32
+RUN = BLOCK // PACK
 LIST_ROWS = 16
 HALF = S // 2
+SCALE_ROW0 = P - K // BLOCK
+W1_SHORT = 128
 V_DIRECT = P // 2
 V_TURNED = V - V_DIRECT
-GROUPS = 4
-LATE = PACK * P
-SCALE_ROW0 = P - 16
-W1_SHORT = 128
-RUN = 8
-RING_BANKS = 8 - GROUPS
+GROUPS = [(2 * P, P), (V_TURNED - P, P // 2), (0, P), (P, P)]
+RING_BANKS = 8 - len(GROUPS)
 
 
 def tile_picked_hop2_gelu_p_kernel(
@@ -59,8 +59,8 @@ def tile_picked_hop2_gelu_p_kernel(
         offs_sb = held([P, S // LIST_ROWS], U16, "offs_sb")
         pos_sb = [held([P, V // LIST_ROWS], U16, "pos%d" % d) for d in range(2)]
         nxt_sb = [held([P, U // LIST_ROWS], U16, "nxt%d" % d) for d in range(2)]
-        words_all = in_slot("late_gates", [P, T], U16, "words_all")
-        scales_all = in_slot("late_terms", [P, T], U8, "scales_all")
+        words_all = in_slot("after_words", [P, T], U16, "words_all")
+        scales_all = in_slot("after_scales", [P, T], U8, "scales_all")
         x_exps = held([P, S], U8, "x_exps")
         w1_cols = [slice(W1_SHORT, H), slice(0, W1_SHORT)]
         short_room = held([P, 2 * P - RUN + PACK * W1_SHORT], F32, "short_room")
@@ -78,28 +78,27 @@ def tile_picked_hop2_gelu_p_kernel(
         nc.sync.dma_start(words_all[:].bitcast(I32), x_words[0].bitcast(I32))
         nc.sync.dma_start(nxt_sb[0][:], nxt1)
         nc.sync.dma_start(nxt_sb[1][:], nxt2)
-        for i in range(2):
-            nc.sync.dma_start(w1_raw[i], w1_rows[:, :, w1_cols[i]])
+        for part in range(2):
+            nc.sync.dma_start(w1_raw[part], w1_rows[:, :, w1_cols[part]])
         nc.sync.dma_start(pos_sb[0][:], pos1)
         nc.sync.dma_start(pos_sb[1][:], pos2)
-        warm = held([P, 2], F32, "warm")
-        nc.gpsimd.memset(warm[:, 0:1], 0.0)
-        nc.scalar.activation(warm[:, 1:2], warm[:, 0:1], ACT.Gelu_apprx_tanh)
         make_identity(nc, ident[:])
+        warm = held([P, 1], F32, "warm")
+        nc.scalar.activation(warm[:], ident[:, 0:1], ACT.Gelu_apprx_tanh)
 
         picked_exps = held([P, S], U8, "picked_exps")
         nc.vector.tensor_copy(picked_exps[:], scales_all[:].indirect(offs_sb[:]))
         for j in range(4):
             nc.sync.dma_start(x_exps[:].bitcast(I32)[j:P:32, :], picked_exps[:].bitcast(I32)[SCALE_ROW0 + j : P : 4, :])
 
-        stage = in_slot("late_terms", [P, 2 * LATE + PACK * N], F32, "stage")
-        both_late = stage[:, : 2 * LATE].rearrange("p (d c) -> p d c", d=2)
-        late = [both_late[:, d, :] for d in range(2)]
-        gate_turned = both_late[:, :, :V_TURNED]
-        w2_raw = stage[:, 2 * LATE :].rearrange("p (t n) -> p t n", t=PACK)
+        stage = in_slot("after_scales", [P, 2 * V + PACK * N], F32, "stage")
+        gate_room = stage[:, : 2 * V].rearrange("p (d c) -> p d c", d=2)
+        gate_turned = gate_room[:, :, :V_TURNED]
+        direct_terms = [gate_room[:, d, : PACK * V_DIRECT] for d in range(2)]
+        w2_raw = stage[:, 2 * V :].rearrange("p (t n) -> p t n", t=PACK)
         gate_rows = gate.rearrange("d p v -> p d v")
         nc.sync.dma_start(gate_turned, gate_rows[:, :, :V_TURNED])
-        w2_rows = w2.rearrange("(q t r) n -> t q r n", t=PACK, r=8)
+        w2_rows = w2.rearrange("(q t r) n -> t q r n", t=PACK, r=RUN)
         for t in range(PACK):
             nc.sync.dma_start(w2_raw[:, t, :], w2_rows[t])
 
@@ -111,13 +110,13 @@ def tile_picked_hop2_gelu_p_kernel(
             staged[:, 5 * P :],
         ]
 
-        def round_w1(copy, t, i):
-            raw = w1_raw[i].rearrange("p j (q t c n) -> p t q c j n", t=PACK, c=2, n=4)
+        def round_w1(copy, t, part):
+            raw = w1_raw[part].rearrange("p j (q t c n) -> p t q c j n", t=PACK, c=2, n=4)
             dst = w1_grouped[t].rearrange("p (q c n j) -> p q c j n", c=2, n=4, j=PACK)
-            copy(dst[:, w1_cols[i].start // 32 : w1_cols[i].stop // 32], raw[:, t])
+            copy(dst[:, w1_cols[part].start // BLOCK : w1_cols[part].stop // BLOCK], raw[:, t])
 
-        for i in range(2):
-            round_w1(nc.scalar.copy, 0, i)
+        for part in range(2):
+            round_w1(nc.scalar.copy, 0, part)
 
         x_codes = []
         for half in range(2):
@@ -128,15 +127,15 @@ def tile_picked_hop2_gelu_p_kernel(
         w1_codes.append(in_slot("w2_grouped", [P, P], U32, "w1_codes3"))
         w1_scales = [held([P, P], U8, "w1_scales%d" % t) for t in range(PACK)]
         quantise(w1_grouped[0], w1_codes[0][:], w1_scales[0][:])
-        for i in range(2):
-            round_w1(nc.scalar.copy, 2, i)
+        for part in range(2):
+            round_w1(nc.scalar.copy, 2, part)
         for t in (1, 3):
-            for i in range(2):
-                round_w1(nc.vector.tensor_copy, t, i)
+            for part in range(2):
+                round_w1(nc.vector.tensor_copy, t, part)
         for t in range(1, PACK):
             quantise(w1_grouped[t], w1_codes[t][:], w1_scales[t][:])
 
-        late_gates = in_slot("late_gates", [P, 2 * V_DIRECT + 2 * U], F32, "late_gates")
+        late_gates = in_slot("after_words", [P, 2 * V_DIRECT + 2 * U], F32, "late_gates")
         gate_direct = late_gates[:, : 2 * V_DIRECT].rearrange("p (d v) -> p d v", d=2)
         gate2_sb = late_gates[:, 2 * V_DIRECT :].rearrange("p (d r) -> p d r", d=2)
         nc.sync.dma_start(gate_direct, gate_rows[:, :, V_TURNED:])
@@ -145,18 +144,15 @@ def tile_picked_hop2_gelu_p_kernel(
         h = []
         for t in range(PACK):
             h_t = held([P, S], F32, "h%d" % t)
-            if t == 0:
-                pieces = [(0, P), (P, P), (2 * P, 2 * P), (4 * P, 2 * P), (6 * P, 2 * P)]
-            else:
-                pieces = [(0, HALF), (HALF, HALF)]
-            for c0, width in pieces:
+            widths = [P, P, 2 * P, 2 * P, 2 * P] if t == 0 else [HALF, HALF]
+            for n, width in enumerate(widths):
+                c0 = sum(widths[:n])
                 acc = bank([P, width])
-                cols = slice(c0 % HALF, c0 % HALF + width)
                 nc.tensor.matmul_mx(
                     out=acc[:],
                     lhsT=w1_codes[t][:].bitcast(FP8X4),
                     lhsT_scale=w1_scales[t][:],
-                    rhs=x_codes[c0 // HALF][:, cols].bitcast(FP4X4),
+                    rhs=x_codes[c0 // HALF][:, c0 % HALF : c0 % HALF + width].bitcast(FP4X4),
                     rhs_scale=x_exps[:, c0 : c0 + width],
                     start=True,
                     stop=True,
@@ -181,10 +177,11 @@ def tile_picked_hop2_gelu_p_kernel(
         z_codes = held([P, V], U32, "z_codes")
         z_scales = held([P, V], U8, "z_scales")
 
-        def second_layer(m, v0, width, acc):
+        def second_layer(m, v0, width):
             cols = slice(v0, v0 + width)
+            acc = bank([P, width])
             nc.tensor.matmul_mx(
-                out=acc,
+                out=acc[:],
                 lhsT=w2_codes[m][:].bitcast(FP8X4),
                 lhsT_scale=w2_scales[m][:],
                 rhs=z_codes[:, cols].bitcast(FP8X4),
@@ -192,29 +189,30 @@ def tile_picked_hop2_gelu_p_kernel(
                 start=True,
                 stop=True,
             )
-            nc.scalar.activation(g[m][:, cols], acc, ACT.Relu)
+            nc.scalar.activation(g[m][:, cols], acc[:], ACT.Relu)
 
-        starts = [2 * P, V_TURNED - P, 0, P]
         last_runs = {0: slice(2 * P, V_TURNED), 2: slice(0, P), 3: slice(P, 2 * P)}
-        z_sum = [psum.tile([P, H], F32, name="z_sum%d" % b) for b in range(GROUPS)]
+        z_sum = [psum.tile([P, H], F32, name="z_sum%d" % b) for b in range(len(GROUPS))]
         z_pairs = [
             [in_slot("pairs%d%d" % (b, u), [P, P], F32, "z_pairs%d%d" % (b, u))[:] for u in range(2)]
-            for b in range(GROUPS)
+            for b in range(len(GROUPS))
         ]
         for t in range(PACK):
-            parts = [held([P, V_TURNED], F32, "part%d_%d" % (t, d))[:] for d in range(2)]
+            turned_terms = [held([P, V_TURNED], F32, "turned_terms%d_%d" % (t, d))[:] for d in range(2)]
             if t < PACK - 1:
                 for d in range(2):
-                    weighted_gather(parts[d], t, d, 0, V_TURNED, gate_turned[:, d, :])
-            for b in range(GROUPS):
+                    weighted_gather(turned_terms[d], t, d, 0, V_TURNED, gate_turned[:, d, :])
+            for b, (v0, fresh) in enumerate(GROUPS):
                 if t == PACK - 1 and b in last_runs:
                     run = last_runs[b]
                     for d in range(2):
-                        weighted_gather(parts[d][:, run], t, d, run.start, run.stop - run.start, gate_turned[:, d, run])
+                        weighted_gather(
+                            turned_terms[d][:, run], t, d, run.start, run.stop - run.start, gate_turned[:, d, run]
+                        )
                 for d in range(2):
                     nc.tensor.matmul(
                         z_sum[b][:, P * t : P * (t + 1)],
-                        parts[d][:, starts[b] : starts[b] + P],
+                        turned_terms[d][:, v0 : v0 + P],
                         ident[:],
                         start=(d == 0),
                         stop=(d == 1),
@@ -231,14 +229,13 @@ def tile_picked_hop2_gelu_p_kernel(
                 quantise(w2_grouped[:, 0, :], w2_codes[0][:], w2_scales[0][:])
                 round_w2(1)
 
-        fresh = [P, P // 2, P, P]
-        words = [in_slot("words%d" % b, [P, 2 * fresh[b]], F32, "words%d" % b)[:] for b in range(GROUPS)]
-        for b in range(GROUPS):
+        z_grouped = [in_slot("grouped%d" % b, [P, 2 * fresh], F32, "z_grouped%d" % b)[:] for b, (v0, fresh) in enumerate(GROUPS)]
+        for b, (v0, fresh) in enumerate(GROUPS):
             turned = bank([P, 2, P])
             for u in range(2):
                 nc.tensor.transpose(turned[:, u, :], z_pairs[b][u], ident[:])
             nc.scalar.copy(
-                words[b].rearrange("p (v u) -> p v u", u=2), turned[:, :, P - fresh[b] :].rearrange("p u v -> p v u")
+                z_grouped[b].rearrange("p (v u) -> p v u", u=2), turned[:, :, P - fresh :].rearrange("p u v -> p v u")
             )
 
         def quantise_z(v0, width, grouped):
@@ -246,29 +243,30 @@ def tile_picked_hop2_gelu_p_kernel(
             quantise(grouped, z_codes[:, cols], z_scales[:, cols])
 
         def quantise_group(b):
-            quantise_z(starts[b] + P - fresh[b], fresh[b], words[b].bitcast(BF16))
+            v0, fresh = GROUPS[b]
+            quantise_z(v0 + P - fresh, fresh, z_grouped[b].bitcast(BF16))
 
         for t in range(PACK):
             for d in range(2):
-                dst = late[d][:, t * V_DIRECT : (t + 1) * V_DIRECT]
+                dst = direct_terms[d][:, t * V_DIRECT : (t + 1) * V_DIRECT]
                 weighted_gather(dst, t, d, V_TURNED, V_DIRECT, gate_direct[:, d, :])
         for b in range(2):
             quantise_group(b)
-        second_layer(0, 2 * P, P, bank([P, P])[:])
-        terms = [late[d][:, : PACK * V_DIRECT].rearrange("p (t c v) -> p c t v", t=PACK, v=4) for d in range(2)]
-        late_grouped = in_slot("pairs21", [P, PACK * V_DIRECT], BF16, "late_grouped")
+        second_layer(0, 2 * P, P)
+        by_fours = [direct_terms[d].rearrange("p (t c v) -> p c t v", t=PACK, v=4) for d in range(2)]
+        direct_grouped = in_slot("pairs21", [P, PACK * V_DIRECT], BF16, "direct_grouped")
         nc.vector.tensor_tensor(
-            late_grouped[:].rearrange("p (c v t) -> p c t v", v=4, t=PACK), terms[0], terms[1], ADD
+            direct_grouped[:].rearrange("p (c v t) -> p c t v", v=4, t=PACK), by_fours[0], by_fours[1], ADD
         )
         quantise_group(2)
-        quantise_z(V_TURNED, V_DIRECT, late_grouped[:])
+        quantise_z(V_TURNED, V_DIRECT, direct_grouped[:])
         quantise_group(3)
         for v0 in (0, 3 * P, P):
-            second_layer(0, v0, P, bank([P, P])[:])
-        w2_codes.append(in_slot("words3", [P, P], U32, "w2_codes1"))
+            second_layer(0, v0, P)
+        w2_codes.append(in_slot("grouped3", [P, P], U32, "w2_codes1"))
         quantise(w2_grouped[:, 1, :], w2_codes[1][:], w2_scales[1][:])
         for v0 in (2 * P, 0):
-            second_layer(1, v0, 2 * P, bank([P, 2 * P])[:])
+            second_layer(1, v0, 2 * P)
 
         roots = []
         for m in range(2):

@@ -21,15 +21,10 @@ ADD = mybir.AluOpType.add
 P = 128
 PACK = 4
 BLOCK = 32
-RUN = BLOCK // PACK
 LIST_ROWS = 16
 HALF = S // 2
 SCALE_ROW0 = P - K // BLOCK
-W1_SHORT = 128
-V_DIRECT = P // 2
-V_TURNED = V - V_DIRECT
-GROUPS = [(2 * P, P), (V_TURNED - P, P // 2), (0, P), (P, P)]
-RING_BANKS = 8 - len(GROUPS)
+V_HALF = V // 2
 
 
 def tile_picked_hop2_gelu_p_kernel(
@@ -48,7 +43,7 @@ def tile_picked_hop2_gelu_p_kernel(
             return shared.tile(shape, dtype, name=name, tag=slot, bufs=1, align_bytes=64)
 
         def bank(shape):
-            return psum.tile(shape, F32, name="bank", tag="bank", bufs=RING_BANKS)
+            return psum.tile(shape, F32, name="bank", tag="bank", bufs=8)
 
         def entries(list_tile, first, count):
             return list_tile[:, first // LIST_ROWS : (first + count) // LIST_ROWS]
@@ -56,18 +51,17 @@ def tile_picked_hop2_gelu_p_kernel(
         def quantise(grouped, codes, scales):
             nc.vector.quantize_mx(out=codes.bitcast(FP8X4), scales=scales, in_=grouped)
 
+        def round_rows(copy, grouped, raw):
+            copy(grouped.rearrange("p (c n j) -> p c j n", n=4, j=PACK), raw.rearrange("p j (c n) -> p c j n", n=4))
+
         offs_sb = held([P, S // LIST_ROWS], U16, "offs_sb")
         pos_sb = [held([P, V // LIST_ROWS], U16, "pos%d" % d) for d in range(2)]
         nxt_sb = [held([P, U // LIST_ROWS], U16, "nxt%d" % d) for d in range(2)]
         words_all = in_slot("after_words", [P, T], U16, "words_all")
         scales_all = in_slot("after_scales", [P, T], U8, "scales_all")
         x_exps = held([P, S], U8, "x_exps")
-        w1_cols = [slice(W1_SHORT, H), slice(0, W1_SHORT)]
-        short_room = held([P, 2 * P - RUN + PACK * W1_SHORT], F32, "short_room")
-        w1_raw = [
-            held([P, PACK, H - W1_SHORT], F32, "w1_long")[:],
-            short_room[:, 2 * P - RUN :].rearrange("p (j n) -> p j n", j=PACK),
-        ]
+        w1_first = held([P, PACK, P], F32, "w1_first")
+        w1_rest = held([P, PACK, H - P], F32, "w1_rest")
         ident = held([P, P], F32, "ident")
 
         nc.vector.memset(scales_all[:].bitcast(I32)[:SCALE_ROW0, :], 0)
@@ -78,9 +72,9 @@ def tile_picked_hop2_gelu_p_kernel(
         nc.sync.dma_start(words_all[:].bitcast(I32), x_words[0].bitcast(I32))
         nc.sync.dma_start(nxt_sb[0][:], nxt1)
         nc.sync.dma_start(nxt_sb[1][:], nxt2)
-        for part in range(2):
-            nc.sync.dma_start(w1_raw[part], w1_rows[:, :, w1_cols[part]])
         nc.sync.dma_start(pos_sb[0][:], pos1)
+        nc.sync.dma_start(w1_first[:], w1_rows[:, :, :P])
+        nc.sync.dma_start(w1_rest[:], w1_rows[:, :, P:])
         nc.sync.dma_start(pos_sb[1][:], pos2)
         make_identity(nc, ident[:])
         warm = held([P, 1], F32, "warm")
@@ -92,53 +86,42 @@ def tile_picked_hop2_gelu_p_kernel(
             nc.sync.dma_start(x_exps[:].bitcast(I32)[j:P:32, :], picked_exps[:].bitcast(I32)[SCALE_ROW0 + j : P : 4, :])
 
         stage = in_slot("after_scales", [P, 2 * V + PACK * N], F32, "stage")
-        gate_room = stage[:, : 2 * V].rearrange("p (d c) -> p d c", d=2)
-        gate_turned = gate_room[:, :, :V_TURNED]
-        direct_terms = [gate_room[:, d, : PACK * V_DIRECT] for d in range(2)]
-        w2_raw = stage[:, 2 * V :].rearrange("p (t n) -> p t n", t=PACK)
-        gate_rows = gate.rearrange("d p v -> p d v")
-        nc.sync.dma_start(gate_turned, gate_rows[:, :, :V_TURNED])
-        w2_rows = w2.rearrange("(q t r) n -> t q r n", t=PACK, r=RUN)
-        for t in range(PACK):
-            nc.sync.dma_start(w2_raw[:, t, :], w2_rows[t])
+        gate_sb = stage[:, : 2 * V].rearrange("p (d c) -> p d c", d=2)
+        w2_raw = stage[:, 2 * V :].rearrange("p (j n) -> p j n", j=PACK)
+        gate_cols = gate.rearrange("d p v -> p d v")
+        nc.sync.dma_start(w2_raw, w2.rearrange("(p j) n -> p j n", j=PACK))
+        for half in range(2):
+            cols = slice(V_HALF * half, V_HALF * (half + 1))
+            nc.sync.dma_start(gate_sb[:, :, cols], gate_cols[:, :, cols])
 
         staged = held([P, 9 * P], BF16, "staged")
-        w1_grouped = [
-            staged[:, 3 * P : 7 * P],
-            staged[:, : 4 * P],
-            short_room[:, : 2 * P].bitcast(BF16),
-            staged[:, 5 * P :],
-        ]
-
-        def round_w1(copy, t, part):
-            raw = w1_raw[part].rearrange("p j (q t c n) -> p t q c j n", t=PACK, c=2, n=4)
-            dst = w1_grouped[t].rearrange("p (q c n j) -> p q c j n", c=2, n=4, j=PACK)
-            copy(dst[:, w1_cols[part].start // BLOCK : w1_cols[part].stop // BLOCK], raw[:, t])
-
-        for part in range(2):
-            round_w1(nc.scalar.copy, 0, part)
-
+        w1_grouped = [staged[:, 3 * P : 7 * P], held([P, PACK * P], BF16, "w1_grouped1"), staged[:, : 4 * P], staged[:, 5 * P :]]
+        w1_codes = [held([P, P], U32, "w1_codes%d" % t) for t in range(PACK)]
+        w1_scales = [held([P, P], U8, "w1_scales%d" % t) for t in range(PACK)]
+        round_rows(nc.scalar.copy, w1_grouped[0][:], w1_first[:])
         x_codes = []
         for half in range(2):
             codes = held([P, HALF], U16, "x_codes%d" % half)
             nc.vector.tensor_copy(codes[:], words_all[:].indirect(entries(offs_sb, HALF * half, HALF)))
             x_codes.append(codes)
-        w1_codes = [held([P, P], U32, "w1_codes%d" % t) for t in range(PACK - 1)]
-        w1_codes.append(in_slot("w2_grouped", [P, P], U32, "w1_codes3"))
-        w1_scales = [held([P, P], U8, "w1_scales%d" % t) for t in range(PACK)]
-        quantise(w1_grouped[0], w1_codes[0][:], w1_scales[0][:])
-        for part in range(2):
-            round_w1(nc.scalar.copy, 2, part)
-        for t in (1, 3):
-            for part in range(2):
-                round_w1(nc.vector.tensor_copy, t, part)
+        quantise(w1_grouped[0][:], w1_codes[0][:], w1_scales[0][:])
+        round_rows(nc.scalar.copy, w1_grouped[1][:], w1_rest[:, :, :P])
+        for t in (2, 3):
+            round_rows(nc.vector.tensor_copy, w1_grouped[t][:], w1_rest[:, :, P * (t - 1) : P * t])
         for t in range(1, PACK):
-            quantise(w1_grouped[t], w1_codes[t][:], w1_scales[t][:])
+            quantise(w1_grouped[t][:], w1_codes[t][:], w1_scales[t][:])
+        w2_grouped = [held([P, PACK * P], BF16, "w2_grouped0")[:], stage[:, V_HALF : V].bitcast(BF16)]
+        w2_codes = [held([P, P], U32, "w2_codes%d" % m) for m in range(2)]
+        w2_scales = [held([P, P], U8, "w2_scales%d" % m) for m in range(2)]
+        round_rows(nc.vector.tensor_copy, w2_grouped[0], w2_raw[:, :, :P])
+        quantise(w2_grouped[0], w2_codes[0][:], w2_scales[0][:])
 
-        late_gates = in_slot("after_words", [P, 2 * V_DIRECT + 2 * U], F32, "late_gates")
-        gate_direct = late_gates[:, : 2 * V_DIRECT].rearrange("p (d v) -> p d v", d=2)
-        gate2_sb = late_gates[:, 2 * V_DIRECT :].rearrange("p (d r) -> p d r", d=2)
-        nc.sync.dma_start(gate_direct, gate_rows[:, :, V_TURNED:])
+        late_gates = in_slot("after_words", [P, 2 * U + 16], F32, "late_gates")
+        gate2_sb = late_gates[:, : 2 * U].rearrange("p (d r) -> p d r", d=2)
+        gate_rows = late_gates[:, 2 * U :].rearrange("p (d k) -> p d k", d=2)[:, :, :2]
+        with nc.allow_non_contiguous_dma(reason="one gate value for each partition"):
+            for d in range(2):
+                nc.sync.dma_start(gate_rows[:, d, :], gate[d, 0, V_HALF:].rearrange("(k v) -> v k", k=2))
         nc.sync.dma_start(gate2_sb, gate2.rearrange("d p r -> p d r"))
 
         h = []
@@ -160,24 +143,78 @@ def tile_picked_hop2_gelu_p_kernel(
                 nc.scalar.activation(h_t[:, c0 : c0 + width], acc[:], ACT.Gelu_apprx_tanh)
             h.append(h_t)
 
-        w2_grouped = in_slot("w2_grouped", [P, 2, PACK * P], BF16, "w2_grouped")
-        w2_codes = [held([P, P], U32, "w2_codes0")]
-        w2_scales = [held([P, P], U8, "w2_scales%d" % m) for m in range(2)]
+        terms = [[held([P, V], F32, "terms%d_%d" % (t, d)) for d in range(2)] for t in range(PACK)]
 
-        def round_w2(m):
-            nc.scalar.copy(
-                w2_grouped[:, m, :].rearrange("p (c n t) -> p c t n", n=4, t=PACK),
-                w2_raw[:, :, P * m : P * (m + 1)].rearrange("p t (c n) -> p c t n", n=4),
+        def gated_gathers(t, v0, width):
+            for d in range(2):
+                nc.vector.tensor_tensor(
+                    terms[t][d][:, v0 : v0 + width],
+                    h[t][:].indirect(entries(pos_sb[d], v0, width)),
+                    gate_sb[:, d, v0 : v0 + width],
+                    MULT,
+                )
+
+        def turn_sum(dst, t, b):
+            for d in range(2):
+                nc.tensor.matmul(
+                    dst, terms[t][d][:, P * b : P * (b + 1)], ident[:], start=(d == 0), stop=(d == 1), is_transpose=True
+                )
+
+        z_rows = [held([P, 2 * P], F32, "z_rows%d" % b) for b in range(4)]
+
+        def z_half(b, u):
+            return z_rows[b][:].bitcast(BF16)[:, 2 * P * u : 2 * P * (u + 1)]
+
+        early = bank([P, 2, 2 * P])
+        for t in range(2):
+            gated_gathers(t, 0, V_HALF)
+            for b in range(2):
+                turn_sum(early[:, b, P * t : P * (t + 1)], t, b)
+        plain = [bank([P, 2, 2 * P]) for b in range(2)]
+        for d in range(2):
+            for t in range(2):
+                nc.scalar.activation(terms[t][d][:, V_HALF:], h[t][:].indirect(entries(pos_sb[d], V_HALF, V_HALF)), ACT.Copy)
+                for k in range(2):
+                    nc.tensor.transpose(
+                        plain[k][:, d, P * t : P * (t + 1)], terms[t][d][:, V_HALF + P * k : V_HALF + P * (k + 1)], ident[:]
+                    )
+            if d == 0:
+                for b in range(2):
+                    nc.scalar.copy(z_half(b, 0), early[:, b, :])
+        scaled = held([P, 2, 2 * P], F32, "scaled")
+        for k in range(2):
+            nc.scalar.activation(scaled[:, k, :], plain[k][:, 0, :], ACT.Copy, scale=gate_rows[:, 0, k : k + 1])
+        late = [bank([P, 2 * P]) for b in range(4)]
+        gated_gathers(2, 0, V)
+        for b in range(4):
+            turn_sum(late[b][:, :P], 2, b)
+        for b in range(4):
+            if b != 1:
+                gated_gathers(3, P * b, 2 * P if b == 0 else P)
+            turn_sum(late[b][:, P:], 3, b)
+        for b in range(4):
+            nc.scalar.copy(z_half(b, 1), late[b][:])
+        for k in range(2):
+            nc.vector.scalar_tensor_tensor(
+                z_half(2 + k, 0), plain[k][:, 1, :], gate_rows[:, 1, k : k + 1], scaled[:, k, :], MULT, ADD
             )
-
-        def weighted_gather(dst, t, d, v0, width, weights):
-            nc.vector.tensor_tensor(dst, h[t][:].indirect(entries(pos_sb[d], v0, width)), weights, MULT)
+        round_rows(nc.vector.tensor_copy, w2_grouped[1], w2_raw[:, :, P:])
 
         g = [held([P, V], F32, "g%d" % m) for m in range(2)]
         z_codes = held([P, V], U32, "z_codes")
         z_scales = held([P, V], U8, "z_scales")
 
-        def second_layer(m, v0, width):
+        def way_back(b):
+            turned = bank([P, 2, P])
+            for w in range(2):
+                source = z_rows[b][:, w : 2 * P : 2]
+                nc.tensor.transpose(turned[:, w, :], source, ident[:])
+            grouped = held([P, P, 2], F32, "z_grouped%d" % b)
+            nc.scalar.copy(grouped[:], turned[:].rearrange("p w v -> p v w"))
+            cols = slice(P * b, P * (b + 1))
+            quantise(grouped[:].rearrange("p v w -> p (v w)").bitcast(BF16), z_codes[:, cols], z_scales[:, cols])
+
+        def second_layer(m, v0, width, on_vector):
             cols = slice(v0, v0 + width)
             acc = bank([P, width])
             nc.tensor.matmul_mx(
@@ -189,93 +226,28 @@ def tile_picked_hop2_gelu_p_kernel(
                 start=True,
                 stop=True,
             )
-            nc.scalar.activation(g[m][:, cols], acc[:], ACT.Relu)
+            if on_vector:
+                nc.vector.tensor_scalar_max(g[m][:, cols], acc[:], 0.0)
+            else:
+                nc.scalar.activation(g[m][:, cols], acc[:], ACT.Relu)
 
-        last_runs = {0: slice(2 * P, V_TURNED), 2: slice(0, P), 3: slice(P, 2 * P)}
-        z_sum = [psum.tile([P, H], F32, name="z_sum%d" % b) for b in range(len(GROUPS))]
-        z_pairs = [
-            [in_slot("pairs%d%d" % (b, u), [P, P], F32, "z_pairs%d%d" % (b, u))[:] for u in range(2)]
-            for b in range(len(GROUPS))
-        ]
-        for t in range(PACK):
-            turned_terms = [held([P, V_TURNED], F32, "turned_terms%d_%d" % (t, d))[:] for d in range(2)]
-            if t < PACK - 1:
-                for d in range(2):
-                    weighted_gather(turned_terms[d], t, d, 0, V_TURNED, gate_turned[:, d, :])
-            for b, (v0, fresh) in enumerate(GROUPS):
-                if t == PACK - 1 and b in last_runs:
-                    run = last_runs[b]
-                    for d in range(2):
-                        weighted_gather(
-                            turned_terms[d][:, run], t, d, run.start, run.stop - run.start, gate_turned[:, d, run]
-                        )
-                for d in range(2):
-                    nc.tensor.matmul(
-                        z_sum[b][:, P * t : P * (t + 1)],
-                        turned_terms[d][:, v0 : v0 + P],
-                        ident[:],
-                        start=(d == 0),
-                        stop=(d == 1),
-                        is_transpose=True,
-                    )
-                if t % 2 == 1:
-                    u = t // 2
-                    nc.scalar.copy(
-                        z_pairs[b][u].bitcast(BF16).rearrange("v (p e) -> v p e", e=2),
-                        z_sum[b][:, 2 * P * u : 2 * P * (u + 1)].rearrange("v (e p) -> v p e", e=2),
-                    )
-            if t == 1:
-                round_w2(0)
-                quantise(w2_grouped[:, 0, :], w2_codes[0][:], w2_scales[0][:])
-                round_w2(1)
+        for b in range(4):
+            way_back(b)
+            if b == 1:
+                quantise(w2_grouped[1], w2_codes[1][:], w2_scales[1][:])
+        for v0, width in ((0, 2 * P), (2 * P, P), (3 * P, P)):
+            for m in range(2):
+                second_layer(m, v0, width, m == 1 and v0 == 3 * P)
 
-        z_grouped = [in_slot("grouped%d" % b, [P, 2 * fresh], F32, "z_grouped%d" % b)[:] for b, (v0, fresh) in enumerate(GROUPS)]
-        for b, (v0, fresh) in enumerate(GROUPS):
-            turned = bank([P, 2, P])
-            for u in range(2):
-                nc.tensor.transpose(turned[:, u, :], z_pairs[b][u], ident[:])
-            nc.scalar.copy(
-                z_grouped[b].rearrange("p (v u) -> p v u", u=2), turned[:, :, P - fresh :].rearrange("p u v -> p v u")
-            )
-
-        def quantise_z(v0, width, grouped):
-            cols = slice(v0, v0 + width)
-            quantise(grouped, z_codes[:, cols], z_scales[:, cols])
-
-        def quantise_group(b):
-            v0, fresh = GROUPS[b]
-            quantise_z(v0 + P - fresh, fresh, z_grouped[b].bitcast(BF16))
-
-        for t in range(PACK):
-            for d in range(2):
-                dst = direct_terms[d][:, t * V_DIRECT : (t + 1) * V_DIRECT]
-                weighted_gather(dst, t, d, V_TURNED, V_DIRECT, gate_direct[:, d, :])
-        for b in range(2):
-            quantise_group(b)
-        second_layer(0, 2 * P, P)
-        by_fours = [direct_terms[d].rearrange("p (t c v) -> p c t v", t=PACK, v=4) for d in range(2)]
-        direct_grouped = in_slot("pairs21", [P, PACK * V_DIRECT], BF16, "direct_grouped")
-        nc.vector.tensor_tensor(
-            direct_grouped[:].rearrange("p (c v t) -> p c t v", v=4, t=PACK), by_fours[0], by_fours[1], ADD
-        )
-        quantise_group(2)
-        quantise_z(V_TURNED, V_DIRECT, direct_grouped[:])
-        quantise_group(3)
-        for v0 in (0, 3 * P, P):
-            second_layer(0, v0, P)
-        w2_codes.append(in_slot("grouped3", [P, P], U32, "w2_codes1"))
-        quantise(w2_grouped[:, 1, :], w2_codes[1][:], w2_scales[1][:])
-        for v0 in (2 * P, 0):
-            second_layer(1, v0, 2 * P)
-
-        roots = []
+        picked = held([P, 2, U], F32, "picked_roots")
+        roots = held([P, 2, 2, U], F32, "roots")
         for m in range(2):
-            for d in range(2):
-                root = held([P, U], F32, "root%d%d" % (m, d))
-                nc.vector.tensor_tensor(root[:], g[m][:].indirect(nxt_sb[d][:]), gate2_sb[:, d, :], MULT)
-                roots.append(root)
-        for m, r0, width in ((0, 0, U), (1, 0, U // 2), (1, U // 2, U // 2)):
+            nc.scalar.activation(picked[:, 1 - m, :], g[1 - m][:].indirect(nxt_sb[0][:]), ACT.Copy)
+            nc.vector.tensor_tensor(roots[:, m, 1, :], g[m][:].indirect(nxt_sb[1][:]), gate2_sb[:, 1, :], MULT)
+        for m in (1, 0):
+            nc.vector.tensor_tensor(roots[:, m, 0, :], picked[:, m, :], gate2_sb[:, 0, :], MULT)
+        for m, r0, width in ((1, 0, U), (0, 0, U // 2), (0, U // 2, U // 2)):
             cols = slice(r0, r0 + width)
             result = held([P, width], F32, "result%d_%d" % (m, r0))
-            nc.vector.tensor_tensor(result[:], roots[2 * m][:, cols], roots[2 * m + 1][:, cols], ADD)
+            nc.vector.tensor_tensor(result[:], roots[:, m, 0, cols], roots[:, m, 1, cols], ADD)
             nc.sync.dma_start(out[P * m : P * (m + 1), cols], result[:])

@@ -61,7 +61,7 @@ def tile_picked_hop2_gelu_p_kernel(
         scales_all = in_slot("after_scales", [P, T], U8, "scales_all")
         x_exps = held([P, S], U8, "x_exps")
         w1_first = held([P, PACK, P], F32, "w1_first")
-        w1_rest = held([P, PACK, H - P], F32, "w1_rest")
+        w1_rest = held([P, PACK, 2 * P], F32, "w1_rest")
         ident = held([P, P], F32, "ident")
 
         nc.vector.memset(scales_all[:].bitcast(I32)[:SCALE_ROW0, :], 0)
@@ -70,51 +70,51 @@ def tile_picked_hop2_gelu_p_kernel(
         nc.sync.dma_start(scales_all[:].bitcast(I32)[SCALE_ROW0:, :], x_scales[0].bitcast(I32))
         nc.sync.dma_start(offs_sb[:], offs)
         nc.sync.dma_start(words_all[:].bitcast(I32), x_words[0].bitcast(I32))
+        nc.sync.dma_start(w1_first[:], w1_rows[:, :, :P])
         nc.sync.dma_start(nxt_sb[0][:], nxt1)
         nc.sync.dma_start(nxt_sb[1][:], nxt2)
         nc.sync.dma_start(pos_sb[0][:], pos1)
-        nc.sync.dma_start(w1_first[:], w1_rows[:, :, :P])
-        nc.sync.dma_start(w1_rest[:], w1_rows[:, :, P:])
+        nc.sync.dma_start(w1_rest[:], w1_rows[:, :, P : 3 * P])
         nc.sync.dma_start(pos_sb[1][:], pos2)
         make_identity(nc, ident[:])
-        warm = held([P, 1], F32, "warm")
-        nc.scalar.activation(warm[:], ident[:, 0:1], ACT.Gelu_apprx_tanh)
+        warm = held([P, 2], F32, "warm")
+        nc.gpsimd.memset(warm[:, 0:1], 0.0)
+        nc.scalar.activation(warm[:, 1:2], warm[:, 0:1], ACT.Gelu_apprx_tanh)
 
         picked_exps = held([P, S], U8, "picked_exps")
         nc.vector.tensor_copy(picked_exps[:], scales_all[:].indirect(offs_sb[:]))
         for j in range(4):
             nc.sync.dma_start(x_exps[:].bitcast(I32)[j:P:32, :], picked_exps[:].bitcast(I32)[SCALE_ROW0 + j : P : 4, :])
 
-        stage = in_slot("after_scales", [P, 2 * V + PACK * N], F32, "stage")
+        stage = in_slot("after_scales", [P, 2 * V + PACK * N + PACK * P], F32, "stage")
         gate_sb = stage[:, : 2 * V].rearrange("p (d c) -> p d c", d=2)
-        w2_raw = stage[:, 2 * V :].rearrange("p (j n) -> p j n", j=PACK)
+        w2_raw = stage[:, 2 * V : 2 * V + PACK * N].rearrange("p (j n) -> p j n", j=PACK)
+        w1_last = stage[:, 2 * V + PACK * N :].rearrange("p (j n) -> p j n", j=PACK)
+        nc.sync.dma_start(w1_last, w1_rows[:, :, 3 * P :])
         gate_cols = gate.rearrange("d p v -> p d v")
-        nc.sync.dma_start(w2_raw, w2.rearrange("(p j) n -> p j n", j=PACK))
         for half in range(2):
             cols = slice(V_HALF * half, V_HALF * (half + 1))
             nc.sync.dma_start(gate_sb[:, :, cols], gate_cols[:, :, cols])
+        nc.sync.dma_start(w2_raw, w2.rearrange("(p j) n -> p j n", j=PACK))
 
-        staged = held([P, 9 * P], BF16, "staged")
-        w1_grouped = [staged[:, 3 * P : 7 * P], held([P, PACK * P], BF16, "w1_grouped1"), staged[:, : 4 * P], staged[:, 5 * P :]]
+        w1_grouped = [in_slot("after_tile0", [P, PACK * P], BF16, "w1_grouped0")]
+        w1_grouped += [held([P, PACK * P], BF16, "w1_grouped%d" % t) for t in range(1, PACK)]
         w1_codes = [held([P, P], U32, "w1_codes%d" % t) for t in range(PACK)]
         w1_scales = [held([P, P], U8, "w1_scales%d" % t) for t in range(PACK)]
         round_rows(nc.scalar.copy, w1_grouped[0][:], w1_first[:])
-        x_codes = []
-        for half in range(2):
-            codes = held([P, HALF], U16, "x_codes%d" % half)
-            nc.vector.tensor_copy(codes[:], words_all[:].indirect(entries(offs_sb, HALF * half, HALF)))
-            x_codes.append(codes)
+        x_codes = [held([P, HALF], U16, "x_codes0")]
+        nc.vector.tensor_copy(x_codes[0][:], words_all[:].indirect(entries(offs_sb, 0, HALF)))
         quantise(w1_grouped[0][:], w1_codes[0][:], w1_scales[0][:])
+        x_codes.append(in_slot("after_tile0", [P, HALF], U16, "x_codes1"))
+        nc.vector.tensor_copy(x_codes[1][:], words_all[:].indirect(entries(offs_sb, HALF, HALF)))
         round_rows(nc.scalar.copy, w1_grouped[1][:], w1_rest[:, :, :P])
-        for t in (2, 3):
-            round_rows(nc.vector.tensor_copy, w1_grouped[t][:], w1_rest[:, :, P * (t - 1) : P * t])
-        for t in range(1, PACK):
+        round_rows(nc.vector.tensor_copy, w1_grouped[2][:], w1_rest[:, :, P:])
+        for t in (1, 2):
             quantise(w1_grouped[t][:], w1_codes[t][:], w1_scales[t][:])
-        w2_grouped = [held([P, PACK * P], BF16, "w2_grouped0")[:], stage[:, V_HALF : V].bitcast(BF16)]
+        round_rows(nc.vector.tensor_copy, w1_grouped[3][:], w1_last)
+        quantise(w1_grouped[3][:], w1_codes[3][:], w1_scales[3][:])
         w2_codes = [held([P, P], U32, "w2_codes%d" % m) for m in range(2)]
         w2_scales = [held([P, P], U8, "w2_scales%d" % m) for m in range(2)]
-        round_rows(nc.vector.tensor_copy, w2_grouped[0], w2_raw[:, :, :P])
-        quantise(w2_grouped[0], w2_codes[0][:], w2_scales[0][:])
 
         late_gates = in_slot("after_words", [P, 2 * U + 16], F32, "late_gates")
         gate2_sb = late_gates[:, : 2 * U].rearrange("p (d r) -> p d r", d=2)
@@ -170,35 +170,43 @@ def tile_picked_hop2_gelu_p_kernel(
             gated_gathers(t, 0, V_HALF)
             for b in range(2):
                 turn_sum(early[:, b, P * t : P * (t + 1)], t, b)
-        plain = [bank([P, 2, 2 * P]) for b in range(2)]
-        for d in range(2):
+        mixed = [bank([P, 2, 2 * P]) for b in range(4)]
+        plain = [[mixed[2 + k][:, 0, :] for k in range(2)], [mixed[k][:, 0, :] for k in range(2)]]
+        late = [mixed[b][:, 1, :] for b in range(4)]
+
+        def plain_gathers(d):
             for t in range(2):
                 nc.scalar.activation(terms[t][d][:, V_HALF:], h[t][:].indirect(entries(pos_sb[d], V_HALF, V_HALF)), ACT.Copy)
                 for k in range(2):
                     nc.tensor.transpose(
-                        plain[k][:, d, P * t : P * (t + 1)], terms[t][d][:, V_HALF + P * k : V_HALF + P * (k + 1)], ident[:]
+                        plain[d][k][:, P * t : P * (t + 1)], terms[t][d][:, V_HALF + P * k : V_HALF + P * (k + 1)], ident[:]
                     )
-            if d == 0:
-                for b in range(2):
-                    nc.scalar.copy(z_half(b, 0), early[:, b, :])
-        scaled = held([P, 2, 2 * P], F32, "scaled")
-        for k in range(2):
-            nc.scalar.activation(scaled[:, k, :], plain[k][:, 0, :], ACT.Copy, scale=gate_rows[:, 0, k : k + 1])
-        late = [bank([P, 2 * P]) for b in range(4)]
+
+        plain_gathers(0)
+        for b in range(2):
+            nc.scalar.copy(z_half(b, 0), early[:, b, :])
         gated_gathers(2, 0, V)
         for b in range(4):
             turn_sum(late[b][:, :P], 2, b)
+        plain_gathers(1)
+        scaled = held([P, 2, 2 * P], F32, "scaled")
+        for k in range(2):
+            nc.scalar.activation(scaled[:, k, :], plain[0][k], ACT.Copy, scale=gate_rows[:, 0, k : k + 1])
         for b in range(4):
             if b != 1:
                 gated_gathers(3, P * b, 2 * P if b == 0 else P)
             turn_sum(late[b][:, P:], 3, b)
         for b in range(4):
-            nc.scalar.copy(z_half(b, 1), late[b][:])
+            nc.scalar.copy(z_half(b, 1), late[b])
         for k in range(2):
             nc.vector.scalar_tensor_tensor(
-                z_half(2 + k, 0), plain[k][:, 1, :], gate_rows[:, 1, k : k + 1], scaled[:, k, :], MULT, ADD
+                z_half(2 + k, 0), plain[1][k], gate_rows[:, 1, k : k + 1], scaled[:, k, :], MULT, ADD
             )
-        round_rows(nc.vector.tensor_copy, w2_grouped[1], w2_raw[:, :, P:])
+        w2_grouped = [scaled[:, m, :].bitcast(BF16) for m in range(2)]
+        for m in range(2):
+            round_rows(nc.vector.tensor_copy, w2_grouped[m], w2_raw[:, :, P * m : P * (m + 1)])
+        for m in range(2):
+            quantise(w2_grouped[m], w2_codes[m][:], w2_scales[m][:])
 
         g = [held([P, V], F32, "g%d" % m) for m in range(2)]
         z_codes = held([P, V], U32, "z_codes")
@@ -233,8 +241,6 @@ def tile_picked_hop2_gelu_p_kernel(
 
         for b in range(4):
             way_back(b)
-            if b == 1:
-                quantise(w2_grouped[1], w2_codes[1][:], w2_scales[1][:])
         for v0, width in ((0, 2 * P), (2 * P, P), (3 * P, P)):
             for m in range(2):
                 second_layer(m, v0, width, m == 1 and v0 == 3 * P)

@@ -170,9 +170,17 @@ def tile_picked_hop2_gelu_p_kernel(
             gated_gathers(t, 0, V_HALF)
             for b in range(2):
                 turn_sum(early[:, b, P * t : P * (t + 1)], t, b)
-        mixed = [bank([P, 2, 2 * P]) for b in range(4)]
-        plain = [[mixed[2 + k][:, 0, :] for k in range(2)], [mixed[k][:, 0, :] for k in range(2)]]
-        late = [mixed[b][:, 1, :] for b in range(4)]
+        mixed = [bank([P, 2, 2 * P]) for k in range(2)]
+        second = bank([P, 2, 2 * P])
+        plain = [[mixed[k][:, 0, :] for k in range(2)], [second[:, k, :] for k in range(2)]]
+        late = [bank([P, 2 * P])[:] for b in range(2)] + [mixed[k][:, 1, :] for k in range(2)]
+
+        def turn_sums(t, groups):
+            for d in range(2):
+                for b in groups:
+                    term = terms[t][d][:, P * b : P * (b + 1)]
+                    dst = late[b][:, P * (t - 2) : P * (t - 1)]
+                    nc.tensor.matmul(dst, term, ident[:], start=(d == 0), stop=(d == 1), is_transpose=True)
 
         def plain_gathers(d):
             for t in range(2):
@@ -186,16 +194,14 @@ def tile_picked_hop2_gelu_p_kernel(
         for b in range(2):
             nc.scalar.copy(z_half(b, 0), early[:, b, :])
         gated_gathers(2, 0, V)
-        for b in range(4):
-            turn_sum(late[b][:, :P], 2, b)
+        turn_sums(2, range(4))
         plain_gathers(1)
         scaled = held([P, 2, 2 * P], F32, "scaled")
         for k in range(2):
             nc.scalar.activation(scaled[:, k, :], plain[0][k], ACT.Copy, scale=gate_rows[:, 0, k : k + 1])
-        for b in range(4):
-            if b != 1:
-                gated_gathers(3, P * b, 2 * P if b == 0 else P)
-            turn_sum(late[b][:, P:], 3, b)
+        for groups in ((0, 1), (2,), (3,)):
+            gated_gathers(3, P * groups[0], P * len(groups))
+            turn_sums(3, groups)
         for b in range(4):
             nc.scalar.copy(z_half(b, 1), late[b])
         for k in range(2):

@@ -69,8 +69,8 @@ def tile_picked_hop2_gelu_p_kernel(
         w1_rows = w1.rearrange("(p j) n -> p j n", j=PACK)
         nc.sync.dma_start(scales_all[:].bitcast(I32)[SCALE_ROW0:, :], x_scales[0].bitcast(I32))
         nc.sync.dma_start(offs_sb[:], offs)
-        nc.sync.dma_start(words_all[:].bitcast(I32), x_words[0].bitcast(I32))
         nc.sync.dma_start(w1_first[:], w1_rows[:, :, :P])
+        nc.sync.dma_start(words_all[:].bitcast(I32), x_words[0].bitcast(I32))
         nc.sync.dma_start(nxt_sb[0][:], nxt1)
         nc.sync.dma_start(nxt_sb[1][:], nxt2)
         nc.sync.dma_start(pos_sb[0][:], pos1)
@@ -97,16 +97,14 @@ def tile_picked_hop2_gelu_p_kernel(
             nc.sync.dma_start(gate_sb[:, :, cols], gate_cols[:, :, cols])
         nc.sync.dma_start(w2_raw, w2.rearrange("(p j) n -> p j n", j=PACK))
 
-        w1_grouped = [in_slot("after_tile0", [P, PACK * P], BF16, "w1_grouped0")]
-        w1_grouped += [held([P, PACK * P], BF16, "w1_grouped%d" % t) for t in range(1, PACK)]
+        w1_grouped = [held([P, PACK * P], BF16, "w1_grouped%d" % t) for t in range(PACK)]
         w1_codes = [held([P, P], U32, "w1_codes%d" % t) for t in range(PACK)]
         w1_scales = [held([P, P], U8, "w1_scales%d" % t) for t in range(PACK)]
         round_rows(nc.scalar.copy, w1_grouped[0][:], w1_first[:])
-        x_codes = [held([P, HALF], U16, "x_codes0")]
-        nc.vector.tensor_copy(x_codes[0][:], words_all[:].indirect(entries(offs_sb, 0, HALF)))
         quantise(w1_grouped[0][:], w1_codes[0][:], w1_scales[0][:])
-        x_codes.append(in_slot("after_tile0", [P, HALF], U16, "x_codes1"))
-        nc.vector.tensor_copy(x_codes[1][:], words_all[:].indirect(entries(offs_sb, HALF, HALF)))
+        x_codes = [held([P, HALF], U16, "x_codes%d" % half) for half in range(2)]
+        for half in range(2):
+            nc.vector.tensor_copy(x_codes[half][:], words_all[:].indirect(entries(offs_sb, HALF * half, HALF)))
         round_rows(nc.scalar.copy, w1_grouped[1][:], w1_rest[:, :, :P])
         round_rows(nc.vector.tensor_copy, w1_grouped[2][:], w1_rest[:, :, P:])
         for t in (1, 2):

from contextlib import ExitStack

import concourse.mybir as mybir
from concourse.masks import make_identity

K, T, S, V, H, N, U = 512, 4096, 1024, 512, 512, 256, 256
FLOPS = 2 * K * H * S + 2 * H * N * V

F32 = mybir.dt.float32
BF16 = mybir.dt.bfloat16
I32 = mybir.dt.int32
U32 = mybir.dt.uint32
U16 = mybir.dt.uint16
U8 = mybir.dt.uint8
FP8X4 = mybir.dt.float8_e4m3fn_x4
FP4X4 = mybir.dt.float4_e2m1fn_x4
ACT = mybir.ActivationFunctionType
MULT = mybir.AluOpType.mult
ADD = mybir.AluOpType.add

P = 128
PACK = 4
BLOCK = 32
LIST_ROWS = 16
HALF = S // 2
SCALE_ROW0 = P - K // BLOCK
V_HALF = V // 2


def tile_picked_hop2_gelu_p_kernel(
    tc, x_words, x_scales, w1, w2, gate, gate2, offs, pos1, pos2, nxt1, nxt2, out
):
    nc = tc.nc
    with ExitStack() as ctx:
        keep = ctx.enter_context(tc.tile_pool(name="keep", bufs=1))
        shared = ctx.enter_context(tc.tile_pool(name="shared", bufs=1))
        psum = ctx.enter_context(tc.psum_pool(name="psum", bufs=1))

        def held(shape, dtype, name):
            return keep.tile(shape, dtype, name=name, align_bytes=64)

        def in_slot(slot, shape, dtype, name):
            return shared.tile(shape, dtype, name=name, tag=slot, bufs=1, align_bytes=64)

        def bank(shape):
            return psum.tile(shape, F32, name="bank", tag="bank", bufs=8)

        def entries(list_tile, first, count):
            return list_tile[:, first // LIST_ROWS : (first + count) // LIST_ROWS]

        def quantise(grouped, codes, scales):
            nc.vector.quantize_mx(out=codes.bitcast(FP8X4), scales=scales, in_=grouped)

        def round_rows(copy, grouped, raw):
            copy(grouped.rearrange("p (c n j) -> p c j n", n=4, j=PACK), raw.rearrange("p j (c n) -> p c j n", n=4))

        offs_sb = held([P, S // LIST_ROWS], U16, "offs_sb")
        pos_sb = [held([P, V // LIST_ROWS], U16, "pos%d" % d) for d in range(2)]
        nxt_sb = [held([P, U // LIST_ROWS], U16, "nxt%d" % d) for d in range(2)]
        words_all = in_slot("after_words", [P, T], U16, "words_all")
        scales_all = in_slot("after_scales", [P, T], U8, "scales_all")
        x_exps = held([P, S], U8, "x_exps")
        w1_first = held([P, PACK, P], F32, "w1_first")
        w1_rest = held([P, PACK, 2 * P], F32, "w1_rest")
        ident = held([P, P], F32, "ident")

        nc.vector.memset(scales_all[:].bitcast(I32)[:SCALE_ROW0, :], 0)
        nc.vector.memset(x_exps[:].bitcast(I32), 0)
        w1_rows = w1.rearrange("(p j) n -> p j n", j=PACK)
        nc.sync.dma_start(scales_all[:].bitcast(I32)[SCALE_ROW0:, :], x_scales[0].bitcast(I32))
        nc.sync.dma_start(offs_sb[:], offs)
        nc.sync.dma_start(w1_first[:], w1_rows[:, :, :P])
        nc.sync.dma_start(words_all[:].bitcast(I32), x_words[0].bitcast(I32))
        nc.sync.dma_start(nxt_sb[0][:], nxt1)
        nc.sync.dma_start(nxt_sb[1][:], nxt2)
        nc.sync.dma_start(pos_sb[0][:], pos1)
        nc.sync.dma_start(w1_rest[:], w1_rows[:, :, P : 3 * P])
        nc.sync.dma_start(pos_sb[1][:], pos2)
        make_identity(nc, ident[:])
        warm = held([P, 2], F32, "warm")
        nc.gpsimd.memset(warm[:, 0:1], 0.0)
        nc.scalar.activation(warm[:, 1:2], warm[:, 0:1], ACT.Gelu_apprx_tanh)

        picked_exps = held([P, S], U8, "picked_exps")
        nc.vector.tensor_copy(picked_exps[:], scales_all[:].indirect(offs_sb[:]))
        for j in range(4):
            nc.sync.dma_start(x_exps[:].bitcast(I32)[j:P:32, :], picked_exps[:].bitcast(I32)[SCALE_ROW0 + j : P : 4, :])

        stage = in_slot("after_scales", [P, 2 * V + PACK * N + PACK * P], F32, "stage")
        gate_sb = stage[:, : 2 * V].rearrange("p (d c) -> p d c", d=2)
        w2_raw = stage[:, 2 * V : 2 * V + PACK * N].rearrange("p (j n) -> p j n", j=PACK)
        w1_last = stage[:, 2 * V + PACK * N :].rearrange("p (j n) -> p j n", j=PACK)
        nc.sync.dma_start(w1_last, w1_rows[:, :, 3 * P :])
        gate_cols = gate.rearrange("d p v -> p d v")
        for half in range(2):
            cols = slice(V_HALF * half, V_HALF * (half + 1))
            nc.sync.dma_start(gate_sb[:, :, cols], gate_cols[:, :, cols])
        nc.sync.dma_start(w2_raw, w2.rearrange("(p j) n -> p j n", j=PACK))

        w1_grouped = [held([P, PACK * P], BF16, "w1_grouped%d" % t) for t in range(PACK)]
        w1_codes = [held([P, P], U32, "w1_codes%d" % t) for t in range(PACK)]
        w1_scales = [held([P, P], U8, "w1_scales%d" % t) for t in range(PACK)]
        round_rows(nc.scalar.copy, w1_grouped[0][:], w1_first[:])
        quantise(w1_grouped[0][:], w1_codes[0][:], w1_scales[0][:])
        x_codes = [held([P, HALF], U16, "x_codes%d" % half) for half in range(2)]
        for half in range(2):
            nc.vector.tensor_copy(x_codes[half][:], words_all[:].indirect(entries(offs_sb, HALF * half, HALF)))
        round_rows(nc.scalar.copy, w1_grouped[1][:], w1_rest[:, :, :P])
        round_rows(nc.vector.tensor_copy, w1_grouped[2][:], w1_rest[:, :, P:])
        for t in (1, 2):
            quantise(w1_grouped[t][:], w1_codes[t][:], w1_scales[t][:])
        round_rows(nc.vector.tensor_copy, w1_grouped[3][:], w1_last)
        quantise(w1_grouped[3][:], w1_codes[3][:], w1_scales[3][:])
        w2_codes = [held([P, P], U32, "w2_codes%d" % m) for m in range(2)]
        w2_scales = [held([P, P], U8, "w2_scales%d" % m) for m in range(2)]

        late_gates = in_slot("after_words", [P, 2 * U + 16], F32, "late_gates")
        gate2_sb = late_gates[:, : 2 * U].rearrange("p (d r) -> p d r", d=2)
        gate_rows = late_gates[:, 2 * U :].rearrange("p (d k) -> p d k", d=2)[:, :, :2]
        with nc.allow_non_contiguous_dma(reason="one gate value for each partition"):
            for d in range(2):
                nc.sync.dma_start(gate_rows[:, d, :], gate[d, 0, V_HALF:].rearrange("(k v) -> v k", k=2))
        nc.sync.dma_start(gate2_sb, gate2.rearrange("d p r -> p d r"))

        h = []
        for t in range(PACK):
            h_t = held([P, S], F32, "h%d" % t)
            widths = [P, P, 2 * P, 2 * P, 2 * P] if t == 0 else [HALF, HALF]
            for n, width in enumerate(widths):
                c0 = sum(widths[:n])
                acc = bank([P, width])
                nc.tensor.matmul_mx(
                    out=acc[:],
                    lhsT=w1_codes[t][:].bitcast(FP8X4),
                    lhsT_scale=w1_scales[t][:],
                    rhs=x_codes[c0 // HALF][:, c0 % HALF : c0 % HALF + width].bitcast(FP4X4),
                    rhs_scale=x_exps[:, c0 : c0 + width],
                    start=True,
                    stop=True,
                )
                nc.scalar.activation(h_t[:, c0 : c0 + width], acc[:], ACT.Gelu_apprx_tanh)
            h.append(h_t)

        terms = [[held([P, V], F32, "terms%d_%d" % (t, d)) for d in range(2)] for t in range(PACK)]

        def gated_gathers(t, v0, width):
            for d in range(2):
                nc.vector.tensor_tensor(
                    terms[t][d][:, v0 : v0 + width],
                    h[t][:].indirect(entries(pos_sb[d], v0, width)),
                    gate_sb[:, d, v0 : v0 + width],
                    MULT,
                )

        def turn_sum(dst, t, b):
            for d in range(2):
                nc.tensor.matmul(
                    dst, terms[t][d][:, P * b : P * (b + 1)], ident[:], start=(d == 0), stop=(d == 1), is_transpose=True
                )

        z_rows = [held([P, 2 * P], F32, "z_rows%d" % b) for b in range(4)]

        def z_half(b, u):
            return z_rows[b][:].bitcast(BF16)[:, 2 * P * u : 2 * P * (u + 1)]

        early = bank([P, 2, 2 * P])
        for t in range(2):
            gated_gathers(t, 0, V_HALF)
            for b in range(2):
                turn_sum(early[:, b, P * t : P * (t + 1)], t, b)
        mixed = [bank([P, 2, 2 * P]) for k in range(2)]
        second = bank([P, 2, 2 * P])
        plain = [[mixed[k][:, 0, :] for k in range(2)], [second[:, k, :] for k in range(2)]]
        late = [bank([P, 2 * P])[:] for b in range(2)] + [mixed[k][:, 1, :] for k in range(2)]

        def turn_sums(t, groups):
            for d in range(2):
                for b in groups:
                    term = terms[t][d][:, P * b : P * (b + 1)]
                    dst = late[b][:, P * (t - 2) : P * (t - 1)]
                    nc.tensor.matmul(dst, term, ident[:], start=(d == 0), stop=(d == 1), is_transpose=True)

        def plain_gathers(d):
            for t in range(2):
                nc.scalar.activation(terms[t][d][:, V_HALF:], h[t][:].indirect(entries(pos_sb[d], V_HALF, V_HALF)), ACT.Copy)
                for k in range(2):
                    nc.tensor.transpose(
                        plain[d][k][:, P * t : P * (t + 1)], terms[t][d][:, V_HALF + P * k : V_HALF + P * (k + 1)], ident[:]
                    )

        plain_gathers(0)
        for b in range(2):
            nc.scalar.copy(z_half(b, 0), early[:, b, :])
        gated_gathers(2, 0, V)
        turn_sums(2, range(4))
        plain_gathers(1)
        scaled = held([P, 2, 2 * P], F32, "scaled")
        for k in range(2):
            nc.scalar.activation(scaled[:, k, :], plain[0][k], ACT.Copy, scale=gate_rows[:, 0, k : k + 1])
        for groups in ((0, 1), (2,), (3,)):
            gated_gathers(3, P * groups[0], P * len(groups))
            turn_sums(3, groups)
        for b in range(4):
            nc.scalar.copy(z_half(b, 1), late[b])
        for k in range(2):
            nc.vector.scalar_tensor_tensor(
                z_half(2 + k, 0), plain[1][k], gate_rows[:, 1, k : k + 1], scaled[:, k, :], MULT, ADD
            )
        w2_grouped = [scaled[:, m, :].bitcast(BF16) for m in range(2)]
        for m in range(2):
            round_rows(nc.vector.tensor_copy, w2_grouped[m], w2_raw[:, :, P * m : P * (m + 1)])
        for m in range(2):
            quantise(w2_grouped[m], w2_codes[m][:], w2_scales[m][:])

        g = [held([P, V], F32, "g%d" % m) for m in range(2)]
        z_codes = held([P, V], U32, "z_codes")
        z_scales = held([P, V], U8, "z_scales")

        def way_back(b):
            turned = bank([P, 2, P])
            for w in range(2):
                source = z_rows[b][:, w : 2 * P : 2]
                nc.tensor.transpose(turned[:, w, :], source, ident[:])
            grouped = held([P, P, 2], F32, "z_grouped%d" % b)
            nc.scalar.copy(grouped[:], turned[:].rearrange("p w v -> p v w"))
            cols = slice(P * b, P * (b + 1))
            quantise(grouped[:].rearrange("p v w -> p (v w)").bitcast(BF16), z_codes[:, cols], z_scales[:, cols])

        def second_layer(m, v0, width, on_vector):
            cols = slice(v0, v0 + width)
            acc = bank([P, width])
            nc.tensor.matmul_mx(
                out=acc[:],
                lhsT=w2_codes[m][:].bitcast(FP8X4),
                lhsT_scale=w2_scales[m][:],
                rhs=z_codes[:, cols].bitcast(FP8X4),
                rhs_scale=z_scales[:, cols],
                start=True,
                stop=True,
            )
            if on_vector:
                nc.vector.tensor_scalar_max(g[m][:, cols], acc[:], 0.0)
            else:
                nc.scalar.activation(g[m][:, cols], acc[:], ACT.Relu)

        for b in range(4):
            way_back(b)
        for v0, width in ((0, 2 * P), (2 * P, P), (3 * P, P)):
            for m in range(2):
                second_layer(m, v0, width, m == 1 and v0 == 3 * P)

        picked = held([P, 2, U], F32, "picked_roots")
        roots = held([P, 2, 2, U], F32, "roots")
        for m in range(2):
            nc.scalar.activation(picked[:, 1 - m, :], g[1 - m][:].indirect(nxt_sb[0][:]), ACT.Copy)
            nc.vector.tensor_tensor(roots[:, m, 1, :], g[m][:].indirect(nxt_sb[1][:]), gate2_sb[:, 1, :], MULT)
        for m in (1, 0):
            nc.vector.tensor_tensor(roots[:, m, 0, :], picked[:, m, :], gate2_sb[:, 0, :], MULT)
        for m, r0, width in ((1, 0, U), (0, 0, U // 2), (0, U // 2, U // 2)):
            cols = slice(r0, r0 + width)
            result = held([P, width], F32, "result%d_%d" % (m, r0))
            nc.vector.tensor_tensor(result[:], roots[:, m, 0, cols], roots[:, m, 1, cols], ADD)
            nc.sync.dma_start(out[P * m : P * (m + 1), cols], result[:])
